import numpy as np, ml_dtypes
CORES = [40,64,80,88,96,104,120,144]
N = 8
import mx_ref
BF = ml_dtypes.bfloat16
def entries(a):
    return np.ascontiguousarray(a.T).reshape(-1)
def table(e):
    return np.ascontiguousarray(np.reshape(e, (-1, 16)).T).astype(np.int32)
def tile(rs):
    return np.stack(rs, axis=2).reshape(128, -1).astype(BF)
def cut(t, i, w=512):
    return t[:, w * i:w * i + w]
def f(rng, *shape):
    return mx_ref.flush((rng.standard_normal(shape, dtype=np.float32) * np.exp2(rng.integers(-2, 3, shape[:-1] + (1,)))).astype(BF))
def wide(rng, *shape, cols=0):
    v = rng.standard_normal(shape, dtype=np.float32) * np.exp2(rng.integers(-12, 13, shape)).astype(np.float32)
    if cols: v *= np.repeat(np.exp2(rng.integers(-cols, cols + 1, shape[:-2] + (1, shape[-1] // 4))) * (rng.random(shape[:-2] + (1, shape[-1] // 4)) > 0.0625), 4, axis=-1).astype(np.float32)
    return mx_ref.flush(v.astype(BF))
T, TG, C1, C2 = 256, 128, 160, 32
def layer(rng, C, M, own=0.25, full=False, hub=False, neg=None):
    snd = np.full((N, N, C), -1); src = np.zeros((N, M, 4), int)
    for s in range(N):
        for r in range(N):
            if s != r and own < 1:
                n = C if full else rng.integers(1, C + 1)
                snd[s, r, rng.permutation(C)[:n]] = rng.choice(T, n, replace=False)
    h, k, c = rng.integers(0, N), rng.integers(0, T), rng.integers(0, C, N)
    if hub:
        for r in range(N):
            if r != h: snd[h, r, c[r]] = k
    for r in range(N):
        src[r] = rng.integers(0, T, (M, 4))
        if own < 1:
            far = T + np.flatnonzero(snd[:, r].reshape(-1) >= 0)
            src[r] = np.where(rng.random((M, 4)) < own, src[r], rng.choice(far, (M, 4)))
        if hub:
            e = k if r == h else T + h * C + c[r]
            src[r][:, 0] = e; src[r][rng.permutation(M)[:M // 4]] = e
            src[r] = rng.permuted(src[r], axis=1)
        if neg is not None:
            bad = np.flatnonzero(np.concatenate([neg[r]] + [(snd[s, r] >= 0) & neg[s][snd[s, r]] for s in range(N)]))
            src[r][rng.permutation(M)[:M // 2]] = rng.choice(bad, (M // 2, 4))
    return np.stack([table(a) for a in snd]), np.stack([table(a) for a in src])
def lists(rng, neg=None, **o):
    a, b = layer(rng, C1, T, neg=neg, **o); c, e = layer(rng, C2, TG, **o)
    return {"snd1": a, "src1": b, "snd2": c, "src2": e}
def setup_inputs(rng):
    return {"x": f(rng, N, 128, 4 * T), "w1": np.repeat(f(rng, 1, 128, 4 * 512), N, axis=0), "w2": np.repeat(f(rng, 1, 128, 512), N, axis=0), **lists(rng)}
def setup_inputs_foreign(rng):
    return {**setup_inputs(rng), **lists(rng, own=0, full=True)}
def setup_inputs_hub(rng):
    return {**setup_inputs(rng), **lists(rng, hub=True)}
def setup_inputs_negative(rng):
    d = setup_inputs(rng)
    neg = np.stack([rng.permutation(T) < T // 2 for r in range(N)])
    v = np.abs(d["x"]).reshape(N, 128, T, 4)
    d["x"] = np.where(neg[:, None, :, None], -v, v).reshape(N, 128, 4 * T)
    d["w1"] = np.abs(d["w1"])
    return {**d, **lists(rng, neg=neg)}
def setup_inputs_self(rng):
    return {**setup_inputs(rng), **lists(rng, own=1)}
def setup_inputs_spread(rng):
    d = setup_inputs(rng); d["x"] = wide(rng, N, 128, 4 * T); return d
def check_inputs(d):
    b = []
    for k in ("w1", "w2"):
        if any(d[k][r].tobytes() != d[k][0].tobytes() for r in range(N)): b.append(k)
    for l, C in (("1", C1), ("2", C2)):
        snd = np.stack([entries(a) for a in d["snd" + l]]).reshape(N, N, C)
        if snd.min() < -1 or snd.max() >= T: b.append("snd" + l)
        for r in range(N):
            if (snd[r, r] != -1).any(): b.append("snd" + l)
            ok = np.concatenate([np.ones(T, bool), snd[:, r].reshape(-1) >= 0])
            e = entries(d["src" + l][r])
            if e.min() < 0 or e.max() >= T + N * C or not ok[e].all(): b.append("src" + l)
    return b
def most(v, snd, src, r, C):
    a = np.concatenate([v[r]] + [v[s][:, entries(snd[s])[r * C:r * C + C]] for s in range(N)], axis=1)
    return a[:, entries(src[r])].reshape(128, -1, 4).max(axis=2)
def reference(x, w1, w2, snd1, src1, snd2, src2):
    q = [mx_ref.quantize(x[r]) for r in range(N)]
    Z = [[mx_ref.matmul(mx_ref.quantize(cut(w1[r], i)), q[r]) for r in range(N)] for i in range(4)]
    U = []
    for r in range(N):
        h = tile([np.maximum(most(Z[i], snd1, src1, r, C1), np.float32(0)) * np.float32(0.05) for i in range(4)])
        U.append(mx_ref.matmul(mx_ref.quantize(w2[r]), mx_ref.quantize(h)))
    return {"y": np.stack([most(U, snd2, src2, r, C2) for r in range(N)])}

@@ -1,0 +1,424 @@
+from concourse.bass import DstId, RemoteDMATransfer
+from concourse.mybir import dt, AluOpType, ActivationFunctionType
+
+N, NT, TG, C1, C2 = 8, 256, 128, 160, 32
+WP = NT + N * C1
+UP = NT + N * C2
+BIG = 1e29
+
+SCRATCH = {
+    "xt": ("sbuf", [128, 4 * NT], "bfloat16"),
+    "w1t": ("sbuf", [128, 2048], "bfloat16"),
+    "w2t": ("sbuf", [128, 512], "bfloat16"),
+    "ls1": ("sbuf", [128, 80], "int32"),
+    "lr1": ("sbuf", [128, 64], "int32"),
+    "ls2": ("sbuf", [128, 16], "int32"),
+    "lr2": ("sbuf", [128, 32], "int32"),
+    "of0": ("sbuf", [128, 80], "uint16"),
+    "of1": ("sbuf", [128, 80], "uint16"),
+    "of2": ("sbuf", [128, 80], "uint16"),
+    "of3": ("sbuf", [128, 80], "uint16"),
+    "or1": ("sbuf", [128, 64], "uint16"),
+    "ti2": ("sbuf", [128, 16], "int32"),
+    "os2": ("sbuf", [128, 14], "uint16"),
+    "or2": ("sbuf", [128, 32], "uint16"),
+    "xg": ("sbuf", [128, 7 * 4 * C1], "bfloat16"),
+    "xgq": ("sbuf", [128, 7 * C1], "float8_e4m3fn_x4"),
+    "xgs": ("sbuf", [128, 7 * C1], "uint8"),
+    "xq": ("sbuf", [128, NT], "float8_e4m3fn_x4"),
+    "xs": ("sbuf", [128, NT], "uint8"),
+    "w1q": ("sbuf", [128, 512], "float8_e4m3fn_x4"),
+    "w1s": ("sbuf", [128, 512], "uint8"),
+    "w2q": ("sbuf", [128, 128], "float8_e4m3fn_x4"),
+    "w2s": ("sbuf", [128, 128], "uint8"),
+    "aq1": ("sbuf", [128, 7 * C1], "float8_e4m3fn_x4"),
+    "as1": ("sbuf", [128, 7 * C1], "uint8"),
+    "aq2": ("sbuf", [128, 7 * C2], "float8_e4m3fn_x4"),
+    "as2": ("sbuf", [128, 7 * C2], "uint8"),
+    "hq1": ("sbuf", [128, C1], "float8_e4m3fn_x4"),
+    "hs1": ("sbuf", [128, C1], "uint8"),
+    "hq2": ("sbuf", [128, 2 * C2], "float8_e4m3fn_x4"),
+    "hs2": ("sbuf", [128, 2 * C2], "uint8"),
+    "wz": ("sbuf", [128, 4 * WP], "bfloat16"),
+    "gt": ("sbuf", [128, 4 * 4 * NT], "bfloat16"),
+    "sc": ("sbuf", [128, 4 * 4 * NT], "bfloat16"),
+    "m1": ("sbuf", [128, 4 * NT], "bfloat16"),
+    "m2": ("sbuf", [128, 2 * TG], "float32"),
+    "hg": ("sbuf", [128, 4 * 256], "bfloat16"),
+    "hgq": ("sbuf", [128, 256], "float8_e4m3fn_x4"),
+    "hgs": ("sbuf", [128, 256], "uint8"),
+    "ht": ("sbuf", [128, 4 * NT], "bfloat16"),
+    "htq": ("sbuf", [128, NT], "float8_e4m3fn_x4"),
+    "hts": ("sbuf", [128, NT], "uint8"),
+    "uz": ("sbuf", [128, UP], "float32"),
+    "gu": ("sbuf", [128, 4 * TG], "float32"),
+    "su": ("sbuf", [128, 4 * TG], "float32"),
+    "yt": ("sbuf", [128, TG], "float32"),
+    "ps": ("psum", [128, 4096], "float32"),
+}
+SEMAPHORES = (["dx", "dw1", "dw2", "ds1", "dr1", "ds2", "dr2", "mz", "mk", "ml", "xo", "w1r", "w2r", "cr1", "ct2", "cs2", "cr2",
+               "sgr", "sgd", "hqr", "hqd", "hc", "hor", "m2o", "m2a", "m2b", "ud", "g2a", "g2b", "sca", "yc", "ys",
+               "sent", "rc1", "rs1", "rc2", "rs2", "gh0", "gh1", "gh2", "gh3a", "gh3b", "sc0", "sc1", "sc2", "sc3"]
+              + ["of%d" % t for t in range(4)] + ["xg%d" % c for c in range(4)] + ["xq%d" % c for c in range(4)]
+              + ["mm%d_%d" % (k, i) for k in range(8) for i in range(4)] + ["fr%d" % k for k in range(8)]
+              + ["arr%d_%d" % (l, s) for l in (1, 2) for s in range(N)])
+
+CHUNKS = ((0, 1), (2, 3), (4,), (5, 6))
+SCALAR = (((0, 0), (0, 1), (1, 0), (1, 1)), ((0, 0), (0, 1), (1, 0), (1, 1), (1, 2)), ((0, 0), (0, 1)),
+          ((0, 0), (0, 1), (1, 0), (1, 1), (1, 2)))
+
+
+def plan(s, T, topo):
+    me = T.cores[s]
+    near = [r for r in range(N) if r == s or topo.may_write(me, T.cores[r])]
+    far = [r for r in range(N) if r not in near]
+    i = near.index(s)
+    relayed = [far[(i + k) % len(far)] for k in range(len(far))]
+    direct = [near[(i + k) % len(near)] for k in range(1, len(near))]
+    help_ = [c for c in topo.cores_of(me) if c != me and all(topo.may_write(c, T.cores[r]) for r in far)]
+    other = [c for c in help_ if topo.die(c) != topo.die(me)]
+    own = [c for c in help_ if topo.die(c) == topo.die(me)]
+    return relayed, direct, (other + own)[:4], own[:2]
+
+
+def bits(es):
+    return sum(1 << e for e in es)
+
+
+def place(s, r):
+    return s if s < r else s - 1
+
+
+DC2 = (slice(0, 4), slice(4, 6), slice(6, 8))
+DS2 = (slice(0, 2), slice(2, 4), slice(4, 8))
+
+
+def landed(layer, s, r, T, topo):
+    relayed, direct, _, _ = plan(s, T, topo)
+    if layer == 1:
+        return 16 if r in relayed or r == direct[0] else 8
+    if r in relayed:
+        return 8
+    j = direct.index(r)
+    return DC2[j].stop - DC2[j].start + DS2[j].stop - DS2[j].start
+
+
+def b8(v):
+    return v.bitcast(dt.uint8)
+
+
+def rank_program(g, core, T, topo):
+    rank = T.rank_of(core)
+    S = T.sem
+    if rank is None:
+        for c in topo.cores_of(core):
+            s = T.rank_of(c)
+            if s is not None:
+                helper(g, core, s, T, topo)
+        return
+    relayed, direct, help1, help2 = plan(rank, T, topo)
+    order = relayed + direct
+    V, P, A, Y = g.vector, g.tensor, g.scalar, g.sync
+    mult, add, mx = AluOpType.mult, AluOpType.add, AluOpType.max
+    COPY, RELU = ActivationFunctionType.Copy, ActivationFunctionType.Relu
+
+    Y.dma_start(T.xt[:], T.x[:]).then_inc(S.dx, 16)
+    for q in range(8):
+        (Y if q < 3 else A).dma_start(T.ls1[16 * q:16 * q + 16, :], T.snd1[:, :]).then_inc(S.ds1, 16)
+    Y.dma_start(T.w1t[:], T.w1[:]).then_inc(S.dw1, 16)
+    for dst, src, sem in ((T.lr1, T.src1, S.dr1), (T.ls2, T.snd2, S.ds2)):
+        for q in range(8):
+            Y.dma_start(dst[16 * q:16 * q + 16, :], src[:, :]).then_inc(sem, 16)
+    Y.dma_start(T.w2t[:], T.w2[:]).then_inc(S.dw2, 16)
+    for q in range(8):
+        Y.dma_start(T.lr2[16 * q:16 * q + 16, :], T.src2[:, :]).then_inc(S.dr2, 16)
+
+    for t in range(4):
+        a = t * WP + NT + rank * C1
+        V.memset(T.wz[:, a:a + C1], 0.0).then_inc(S.mz, 1)
+    V.memset(T.uz[:, NT + rank * C2:NT + rank * C2 + C2], 0.0).then_inc(S.mz, 1)
+    V.memset(T.hg[:, 4 * 7 * C2:1024], 0.0).then_inc(S.mz, 1)
+    V.memset(T.m1[:], 1.0).then_inc(S.mk, 1)
+    V.memset(T.m2[:], BIG).then_inc(S.mk, 1)
+    V.wait_ge(S.mk, 2)
+    V.memset(T.m1[:, 0:4 * NT:4], 0.0).then_inc(S.ml, 1)
+    V.memset(T.m2[:, 0:2 * TG:4], -BIG).then_inc(S.ml, 1)
+
+    V.wait_ge(S.ds1, 128)
+    V.tensor_scalar(T.of0[:], T.ls1[:], 4, 0, mult, mx).then_inc(S.of0, 1)
+    V.wait_ge(S.of0, 1)
+    for t in (1, 2, 3):
+        V.tensor_scalar(T["of%d" % t][:], T.of0[:], t, None, add).then_inc(S["of%d" % t], 1)
+
+    def pick(eng, pos, t, sem):
+        r = order[pos]
+        out = T.xg[:, 4 * C1 * pos + t:4 * C1 * (pos + 1):4]
+        win = T.xt[:, :].indirect(T["of%d" % t][:, 10 * r:10 * r + 10])
+        if eng is V:
+            V.tensor_copy(out, win).then_inc(sem, 1)
+        else:
+            A.activation(out, win, COPY).then_inc(sem, 1)
+
+    A.wait_ge(S.dx, 16)
+    A.wait_ge(S.of0, 1)
+    A.wait_ge(S.of1, 1)
+    V.wait_ge(S.dx, 16)
+    for t in (1, 2, 3):
+        V.wait_ge(S["of%d" % t], 1)
+    for c, chunk in enumerate(CHUNKS):
+        sem = S["xg%d" % c]
+        if c == 1:
+            A.wait_ge(S.of2, 1)
+        for j, t in SCALAR[c]:
+            pick(A, chunk[j], t, sem)
+        for j in range(len(chunk)):
+            for t in range(4):
+                if (j, t) not in SCALAR[c]:
+                    pick(V, chunk[j], t, sem)
+        V.wait_ge(sem, 4 * len(chunk))
+        a, b = C1 * chunk[0], C1 * (chunk[-1] + 1)
+        V.quantize_mx(T.xgq[:, a:b], T.xgs[:, a:b], T.xg[:, 4 * a:4 * b]).then_inc(S["xq%d" % c], 1)
+
+    V.quantize_mx(T.xq[:], T.xs[:], T.xt[:]).then_inc(S.xo, 1)
+    V.wait_ge(S.dw1, 16)
+    V.quantize_mx(T.w1q[:], T.w1s[:], T.w1t[:]).then_inc(S.w1r, 1)
+    V.wait_ge(S.dr1, 128)
+    V.tensor_copy(T.or1[:], T.lr1[:]).then_inc(S.cr1, 1)
+    V.wait_ge(S.ds2, 128)
+    V.tensor_scalar(T.ti2[:], T.ls2[:], 4, 3, mult, add).then_inc(S.ct2, 1)
+    V.wait_ge(S.ct2, 1)
+    for pos, r in enumerate(order):
+        V.tensor_scalar(T.os2[:, 2 * pos:2 * pos + 2], T.ti2[:, 2 * r:2 * r + 2], 0, None, mx).then_inc(S.cs2, 1)
+    V.wait_ge(S.dw2, 16)
+    V.quantize_mx(T.w2q[:], T.w2s[:], T.w2t[:]).then_inc(S.w2r, 1)
+    V.wait_ge(S.dr2, 128)
+    V.tensor_copy(T.or2[:], T.lr2[:]).then_inc(S.cr2, 1)
+
+    def rankof(way, p):
+        for s in range(N):
+            if s != rank:
+                rl, di, _, _ = plan(s, T, topo)
+                if (rl if way == "r" else di)[p] == rank:
+                    return s
+
+    srcs = [rankof(w, p) for w, p in (("r", 0), ("r", 1), ("d", 0), ("r", 2), ("r", 3), ("d", 1), ("d", 2))]
+    P.wait_ge(S.w1r, 1)
+    for k in range(8):
+        if k == 0:
+            P.wait_ge(S.xo, 1)
+            n, base, mq, ms = NT, 0, T.xq[:], T.xs[:]
+        else:
+            s = srcs[k - 1]
+            P.wait_ge(S["arr1_%d" % s], landed(1, s, rank, T, topo))
+            a = C1 * place(s, rank)
+            n, base, mq, ms = C1, NT + C1 * s, T.aq1[:, a:a + C1], T.as1[:, a:a + C1]
+        if k >= 2:
+            P.wait_ge(S["fr%d" % (k - 2)], 4)
+        for i in (0, 2, 1, 3):
+            bank = 512 * (4 * (k % 2) + i)
+            done = S["mm%d_%d" % (k, i)]
+            P.matmul_mx(T.ps[:, bank:bank + n], T.w1q[:, 128 * i:128 * i + 128], T.w1s[:, 128 * i:128 * i + 128],
+                        mq, ms, True, True).then_inc(done, 1)
+            out, res = T.wz[:, WP * i + base:WP * i + base + n], T.ps[:, bank:bank + n]
+            if i < 2:
+                V.wait_ge(done, 1)
+                V.tensor_scalar(out, res, 0.05, 0.0, mult, mx).then_inc(S["fr%d" % k], 1)
+            else:
+                A.wait_ge(done, 1)
+                A.activation(out, res, RELU, scale=0.05).then_inc(S["fr%d" % k], 1)
+
+    for e in (V, A):
+        e.wait_ge(S.mz, 6)
+        e.wait_ge(S.cr1, 1)
+        e.wait_ge(S.fr6, 4)
+        e.wait_ge(S.fr7, 4)
+    V.wait_ge(S.ml, 2)
+    V.wait_ge(S.cs2, 7)
+
+    def sources(eng, t, h, sem):
+        out = T.gt[:, 1024 * t + 512 * h:1024 * t + 512 * h + 512]
+        win = T.wz[:, WP * t:WP * (t + 1)].indirect(T.or1[:, 32 * h:32 * h + 32])
+        if eng is V:
+            V.tensor_copy(out, win).then_inc(sem, 1)
+        else:
+            A.activation(out, win, COPY).then_inc(sem, 1)
+
+    def scan(t, a, b):
+        o = 1024 * t
+        V.tensor_tensor_scan(T.sc[:, o + a:o + b], T.m1[:, a:b], T.gt[:, o + a:o + b], 0.0, mult, mx).then_inc(S["sc%d" % t], 1)
+
+    def chosen(t, a, b, sem):
+        V.tensor_copy(T.hg[:, 4 * a + t:4 * b:4],
+                      T.sc[:, 1024 * t:1024 * t + 1024].indirect(T.os2[:, a // 16:b // 16])).then_inc(sem, 1)
+
+    sources(A, 0, 0, S.gh0)
+    sources(A, 1, 0, S.gh1)
+    sources(A, 2, 0, S.gh2)
+    sources(A, 2, 1, S.gh2)
+    sources(A, 3, 0, S.gh3a)
+    sources(A, 3, 1, S.gh3b)
+
+    sources(V, 0, 1, S.gh0)
+    V.wait_ge(S.gh0, 2)
+    scan(0, 0, 1024)
+    sources(V, 1, 1, S.gh1)
+    V.wait_ge(S.gh1, 2)
+    scan(1, 0, 1024)
+    V.wait_ge(S.sc0, 1)
+    chosen(0, 0, 7 * C2, S.sgr)
+    V.wait_ge(S.sc1, 1)
+    chosen(1, 0, 7 * C2, S.sgr)
+    V.wait_ge(S.gh2, 2)
+    scan(2, 0, 1024)
+    V.wait_ge(S.sc2, 1)
+    chosen(2, 0, 7 * C2, S.sgr)
+    V.wait_ge(S.gh3a, 1)
+    scan(3, 0, 512)
+    V.wait_ge(S.gh3b, 1)
+    scan(3, 512, 1024)
+    V.wait_ge(S.sc3, 2)
+    chosen(3, 0, 128, S.sgr)
+    V.wait_ge(S.sgr, 4)
+    V.quantize_mx(T.hgq[:, 0:128], T.hgs[:, 0:128], T.hg[:, 0:512]).then_inc(S.hqr, 1)
+    chosen(3, 128, 7 * C2, S.sgd)
+    V.wait_ge(S.sgd, 1)
+    V.quantize_mx(T.hgq[:, 128:256], T.hgs[:, 128:256], T.hg[:, 512:1024]).then_inc(S.hqd, 1)
+
+    for t in range(4):
+        A.wait_ge(S["sc%d" % t], 2 if t == 3 else 1)
+        A.activation(T.ht[:, t:4 * NT:4], T.sc[:, 1024 * t + 3:1024 * t + 1024:4], COPY).then_inc(S.hc, 1)
+    V.wait_ge(S.hc, 4)
+    V.quantize_mx(T.htq[:], T.hts[:], T.ht[:]).then_inc(S.hor, 1)
+
+    P.wait_ge(S.w2r, 1)
+    P.wait_ge(S.hor, 1)
+    P.matmul_mx(T.ps[:, 0:NT], T.w2q[:], T.w2s[:], T.htq[:], T.hts[:], True, True).then_inc(S.m2o, 1)
+    V.wait_ge(S.m2o, 1)
+    V.tensor_copy(T.uz[:, 0:NT], T.ps[:, 0:NT]).then_inc(S.ud, 1)
+    for s in range(N):
+        if s != rank:
+            P.wait_ge(S["arr2_%d" % s], landed(2, s, rank, T, topo))
+    P.matmul_mx(T.ps[:, 2048:2176], T.w2q[:], T.w2s[:], T.aq2[:, 0:128], T.as2[:, 0:128], True, True).then_inc(S.m2a, 1)
+    P.matmul_mx(T.ps[:, 2560:2688], T.w2q[:], T.w2s[:], T.aq2[:, 96:224], T.as2[:, 96:224], True, True).then_inc(S.m2b, 1)
+    V.wait_ge(S.m2a, 1)
+    A.wait_ge(S.m2b, 1)
+    done, hole = 1, C2 * rank
+    for a, b, bank in ((0, 112, 2048), (112, 224, 2560 - 96)):
+        for lo, hi in ((a, min(b, hole)), (max(a, hole), b)):
+            if lo < hi:
+                o = NT + lo + (C2 if lo >= hole else 0)
+                out, res = T.uz[:, o:o + hi - lo], T.ps[:, bank + lo:bank + hi]
+                if a == 0:
+                    V.tensor_copy(out, res).then_inc(S.ud, 1)
+                else:
+                    A.activation(out, res, COPY).then_inc(S.ud, 1)
+                done += 1
+
+    V.wait_ge(S.cr2, 1)
+    A.wait_ge(S.cr2, 1)
+    V.wait_ge(S.ud, done)
+    A.wait_ge(S.ud, done)
+    V.tensor_copy(T.gu[:, 0:256], T.uz[:, :].indirect(T.or2[:, 0:16])).then_inc(S.g2a, 1)
+    A.activation(T.gu[:, 256:512], T.uz[:, :].indirect(T.or2[:, 16:32]), COPY).then_inc(S.g2b, 1)
+    for h, sem in ((0, S.g2a), (256, S.g2b)):
+        V.wait_ge(sem, 1)
+        V.tensor_tensor_scan(T.su[:, h:h + 256], T.m2[:], T.gu[:, h:h + 256], 0.0, AluOpType.min, mx).then_inc(S.sca, 1)
+    V.wait_ge(S.sca, 2)
+    V.tensor_copy(T.yt[:], T.su[:, 3:4 * TG:4]).then_inc(S.yc, 1)
+    Y.wait_ge(S.yc, 1)
+    Y.dma_start(T.y[:], T.yt[:]).then_inc(S.ys, 16)
+    Y.wait_ge(S.ys, 16)
+
+    sent = [0]
+
+    def fused(parts):
+        ts = []
+        for d, es, src, dst, sem in parts:
+            rid, pid = topo.addr(d, core)
+            ts.append(RemoteDMATransfer(dst_ids=[DstId(rid=rid, pnc=pid)], dma_engine_mask=bits(es), remote_sem=sem,
+                                        src=src, dst=dst))
+            sent[0] += len(es)
+        g.remote_dma_fused(ts, local_sem=S.sent)
+
+    for c, chunk in enumerate(CHUNKS):
+        g.wait_ge(S["xq%d" % c], 1)
+        codes, planes = [], []
+        for j, pos in enumerate(chunk):
+            a = C1 * pos
+            r = order[pos]
+            d = help1[pos] if pos < 4 else T.cores[r]
+            es = topo.engines(core, d)
+            w = len(es) // len(chunk)
+            es = es[w * j:w * j + w]
+            sq, ss = b8(T.xgq[:, a:a + C1]), T.xgs[:, a:a + C1]
+            if pos < 4:
+                codes.append((d, es, sq, b8(T.hq1[:, :]), S.rc1))
+                planes.append((d, es, ss, T.hs1[:, :], S.rs1))
+            else:
+                o = C1 * place(rank, r)
+                sem = S["arr1_%d" % rank]
+                codes.append((d, es, sq, b8(T.aq1[:, o:o + C1]), sem))
+                planes.append((d, es, ss, T.as1[:, o:o + C1], sem))
+        fused(codes)
+        fused(planes)
+
+    g.wait_ge(S.hqr, 1)
+    codes, planes = [], []
+    for j, d in enumerate(help2):
+        es = topo.engines(core, d)
+        es = es[len(es) // 2 * j:len(es) // 2 * (j + 1)]
+        a = 2 * C2 * j
+        codes.append((d, es, b8(T.hgq[:, a:a + 2 * C2]), b8(T.hq2[:, :]), S.rc2))
+        planes.append((d, es, T.hgs[:, a:a + 2 * C2], T.hs2[:, :], S.rs2))
+    fused(codes)
+    fused(planes)
+    g.wait_ge(S.hqd, 1)
+    codes, planes = [], []
+    for j, r in enumerate(direct):
+        d = T.cores[r]
+        es = topo.engines(core, d)
+        a, o = C2 * (4 + j), C2 * place(rank, r)
+        sem = S["arr2_%d" % rank]
+        codes.append((d, es[DC2[j]], b8(T.hgq[:, a:a + C2]), b8(T.aq2[:, o:o + C2]), sem))
+        planes.append((d, es[DS2[j]], T.hgs[:, a:a + C2], T.as2[:, o:o + C2], sem))
+    fused(codes)
+    fused(planes)
+    g.wait_ge(S.sent, sent[0])
+
+
+def helper(g, core, s, T, topo):
+    relayed, _, help1, help2 = plan(s, T, topo)
+    S = T.sem
+    me = T.cores[s]
+    sent = 0
+    if core in help1:
+        j = help1.index(core)
+        w = len(topo.engines(me, core)) // 2
+        r = relayed[j]
+        d = T.cores[r]
+        o = C1 * place(s, r)
+        rid, pid = topo.addr(d, core)
+        for sem, out, src in ((S.rc1, b8(T.aq1[:, o:o + C1]), b8(T.hq1[:, :])), (S.rs1, T.as1[:, o:o + C1], T.hs1[:, :])):
+            g.wait_ge(sem, w)
+            g.remote_dma(out, src, S["arr1_%d" % s], S.sent, pid, rid, topo.mask(core, d))
+            sent += len(topo.engines(core, d))
+    if core in help2:
+        j = help2.index(core)
+        w = len(topo.engines(me, core)) // 2
+        two = relayed[2 * j:2 * j + 2]
+        for sem, code in ((S.rc2, True), (S.rs2, False)):
+            g.wait_ge(sem, w)
+            ts = []
+            for i, r in enumerate(two):
+                d = T.cores[r]
+                es = topo.engines(core, d)[4 * i:4 * i + 4]
+                o, a = C2 * place(s, r), C2 * i
+                src = b8(T.hq2[:, a:a + C2]) if code else T.hs2[:, a:a + C2]
+                dst = b8(T.aq2[:, o:o + C2]) if code else T.as2[:, o:o + C2]
+                rid, pid = topo.addr(d, core)
+                ts.append(RemoteDMATransfer(dst_ids=[DstId(rid=rid, pnc=pid)], dma_engine_mask=bits(es),
+                                            remote_sem=S["arr2_%d" % s], src=src, dst=dst))
+                sent += len(es)
+            g.remote_dma_fused(ts, local_sem=S.sent)
+    if sent:
+        g.wait_ge(S.sent, sent)

@@ -4,24 +4,21 @@ from concourse.mybir import dt, AluOpType, ActivationFunctionType
 N, NT, TG, C1, C2 = 8, 256, 128, 160, 32
 WP = NT + N * C1
 UP = NT + N * C2
-BIG = 1e29
+PAD = 16
+O1E, O2E, OS2, OEND = 0, 64, 96, 110
 
 SCRATCH = {
-    "xt": ("sbuf", [128, 4 * NT], "bfloat16"),
+    "xt": ("sbuf", [128, PAD + 4 * NT], "bfloat16"),
     "w1t": ("sbuf", [128, 2048], "bfloat16"),
     "w2t": ("sbuf", [128, 512], "bfloat16"),
     "ls1": ("sbuf", [128, 80], "int32"),
-    "lr1": ("sbuf", [128, 64], "int32"),
+    "lsrc": ("sbuf", [128, 388], "int32"),
     "ls2": ("sbuf", [128, 16], "int32"),
-    "lr2": ("sbuf", [128, 32], "int32"),
+    "ol": ("sbuf", [128, 112], "uint16"),
     "of0": ("sbuf", [128, 80], "uint16"),
     "of1": ("sbuf", [128, 80], "uint16"),
     "of2": ("sbuf", [128, 80], "uint16"),
     "of3": ("sbuf", [128, 80], "uint16"),
-    "or1": ("sbuf", [128, 64], "uint16"),
-    "ti2": ("sbuf", [128, 16], "int32"),
-    "os2": ("sbuf", [128, 14], "uint16"),
-    "or2": ("sbuf", [128, 32], "uint16"),
     "xg": ("sbuf", [128, 7 * 4 * C1], "bfloat16"),
     "xgq": ("sbuf", [128, 7 * C1], "float8_e4m3fn_x4"),
     "xgs": ("sbuf", [128, 7 * C1], "uint8"),
@@ -35,15 +32,15 @@ SCRATCH = {
     "as1": ("sbuf", [128, 7 * C1], "uint8"),
     "aq2": ("sbuf", [128, 7 * C2], "float8_e4m3fn_x4"),
     "as2": ("sbuf", [128, 7 * C2], "uint8"),
-    "hq1": ("sbuf", [128, C1], "float8_e4m3fn_x4"),
-    "hs1": ("sbuf", [128, C1], "uint8"),
+    "hq1": ("sbuf", [128, 2 * C1], "float8_e4m3fn_x4"),
+    "hs1": ("sbuf", [128, 2 * C1], "uint8"),
     "hq2": ("sbuf", [128, 2 * C2], "float8_e4m3fn_x4"),
     "hs2": ("sbuf", [128, 2 * C2], "uint8"),
     "wz": ("sbuf", [128, 4 * WP], "bfloat16"),
-    "gt": ("sbuf", [128, 4 * 4 * NT], "bfloat16"),
-    "sc": ("sbuf", [128, 4 * 4 * NT], "bfloat16"),
-    "m1": ("sbuf", [128, 4 * NT], "bfloat16"),
-    "m2": ("sbuf", [128, 2 * TG], "float32"),
+    "mx": ("sbuf", [128, 16 * NT], "bfloat16"),
+    "gt": ("sbuf", [128, 2 * 3 * NT], "bfloat16"),
+    "sc": ("sbuf", [128, 2 * 3 * NT], "bfloat16"),
+    "m1": ("sbuf", [128, 3 * NT], "bfloat16"),
     "hg": ("sbuf", [128, 4 * 256], "bfloat16"),
     "hgq": ("sbuf", [128, 256], "float8_e4m3fn_x4"),
     "hgs": ("sbuf", [128, 256], "uint8"),
@@ -52,20 +49,22 @@ SCRATCH = {
     "hts": ("sbuf", [128, NT], "uint8"),
     "uz": ("sbuf", [128, UP], "float32"),
     "gu": ("sbuf", [128, 4 * TG], "float32"),
-    "su": ("sbuf", [128, 4 * TG], "float32"),
     "yt": ("sbuf", [128, TG], "float32"),
     "ps": ("psum", [128, 4096], "float32"),
 }
-SEMAPHORES = (["dx", "dw1", "dw2", "ds1", "dr1", "ds2", "dr2", "mz", "mk", "ml", "xo", "w1r", "w2r", "cr1", "ct2", "cs2", "cr2",
-               "sgr", "sgd", "hqr", "hqd", "hc", "hor", "m2o", "m2a", "m2b", "ud", "g2a", "g2b", "sca", "yc", "ys",
-               "sent", "rc1", "rs1", "rc2", "rs2", "gh0", "gh1", "gh2", "gh3a", "gh3b", "sc0", "sc1", "sc2", "sc3"]
-              + ["of%d" % t for t in range(4)] + ["xg%d" % c for c in range(4)] + ["xq%d" % c for c in range(4)]
-              + ["mm%d_%d" % (k, i) for k in range(8) for i in range(4)] + ["fr%d" % k for k in range(8)]
+SEMAPHORES = (["dx", "dw1", "dw2", "ds1", "dl", "dr", "mz", "mp", "mk", "ml", "xo", "w1a", "w1b", "w2r", "lo",
+               "cf", "cd", "hqr", "hqd", "hc", "hor", "m2o", "m2a", "m2b", "ud", "yc", "ys",
+               "sent", "rc1a", "rs1a", "rc1b", "rs1b", "r2", "r2s", "lq", "g2", "g3"]
+              + ["of%d" % t for t in range(4)] + ["xg%d" % c for c in range(7)] + ["xq%d" % c for c in range(7)]
+              + ["mm%d_%d" % (i, b) for i in range(4) for b in range(2)]
+              + ["fr%d_%d" % (i, b) for i in range(4) for b in range(2)]
+              + ["f%d_%d" % (t, e) for t in range(4) for e in range(4) if t < 2 or e > 1] + ["u%d" % e for e in range(4)]
               + ["arr%d_%d" % (l, s) for l in (1, 2) for s in range(N)])
 
-CHUNKS = ((0, 1), (2, 3), (4,), (5, 6))
-SCALAR = (((0, 0), (0, 1), (1, 0), (1, 1)), ((0, 0), (0, 1), (1, 0), (1, 1), (1, 2)), ((0, 0), (0, 1)),
-          ((0, 0), (0, 1), (1, 0), (1, 1), (1, 2)))
+VECTOR_GATHERS = (2, 2, 2, 1, 2, 1, 2)
+CODE_CALLS = ((0, 1), (2, 3), (4,), (5,), (6,))
+PLANE_CALLS = ((0, 1), (2, 3), (4,), (5,), (6,))
+EXPECTED = ((0,), (1,), (4,), (2,), (5,), (3,), (6,))
 
 
 def plan(s, T, topo):
@@ -78,7 +77,7 @@ def plan(s, T, topo):
     help_ = [c for c in topo.cores_of(me) if c != me and all(topo.may_write(c, T.cores[r]) for r in far)]
     other = [c for c in help_ if topo.die(c) != topo.die(me)]
     own = [c for c in help_ if topo.die(c) == topo.die(me)]
-    return relayed, direct, (other + own)[:4], own[:2]
+    return relayed, direct, (2 * other[:2], 2 * own[:2]), (own[:2], other[:2])
 
 
 def bits(es):
@@ -89,14 +88,27 @@ def place(s, r):
     return s if s < r else s - 1
 
 
+def place1(pos):
+    return [p for group in EXPECTED for p in group].index(pos)
+
+
+def share(es, calls, pos):
+    call = [c for c in calls if pos in c][0]
+    w, j = len(es) // len(call), call.index(pos)
+    return es[w * j:w * j + w]
+
+
 DC2 = (slice(0, 4), slice(4, 6), slice(6, 8))
 DS2 = (slice(0, 2), slice(2, 4), slice(4, 8))
 
 
 def landed(layer, s, r, T, topo):
-    relayed, direct, _, _ = plan(s, T, topo)
+    relayed, direct, help1, _ = plan(s, T, topo)
     if layer == 1:
-        return 16 if r in relayed or r == direct[0] else 8
+        if r in relayed:
+            return sum(len(topo.engines(h[relayed.index(r)], T.cores[r])) for h in help1)
+        es = topo.engines(T.cores[s], T.cores[r])
+        return sum(len(share(es, calls, 4 + direct.index(r))) for calls in (CODE_CALLS, PLANE_CALLS))
     if r in relayed:
         return 8
     j = direct.index(r)
@@ -105,6 +117,16 @@ def landed(layer, s, r, T, topo):
 
 def b8(v):
     return v.bitcast(dt.uint8)
+
+
+def runs(order):
+    out = []
+    for p, r in enumerate(order):
+        if out and out[-1][1] + out[-1][2] == r:
+            out[-1][2] += 1
+        else:
+            out.append([p, r, 1])
+    return out
 
 
 def rank_program(g, core, T, topo):
@@ -121,175 +143,188 @@ def rank_program(g, core, T, topo):
     V, P, A, Y = g.vector, g.tensor, g.scalar, g.sync
     mult, add, mx = AluOpType.mult, AluOpType.add, AluOpType.max
     COPY, RELU = ActivationFunctionType.Copy, ActivationFunctionType.Relu
+    seen = {}
 
-    Y.dma_start(T.xt[:], T.x[:]).then_inc(S.dx, 16)
-    for q in range(8):
-        (Y if q < 3 else A).dma_start(T.ls1[16 * q:16 * q + 16, :], T.snd1[:, :]).then_inc(S.ds1, 16)
+    def need(eng, name, sem, n):
+        if seen.get((name, sem), 0) < n:
+            eng.wait_ge(S[sem], n)
+            seen[(name, sem)] = n
+
+    def gather(eng, out, win, sem):
+        if eng is V:
+            V.tensor_copy(out, win).then_inc(S[sem], 1)
+        else:
+            A.activation(out, win, COPY).then_inc(S[sem], 1)
+
+    for q, e in enumerate((A, Y)):
+        e.dma_start(T.ls1[16 * q:16 * q + 16, :], T.snd1[:, :]).then_inc(S.ds1, 16)
+    Y.dma_start(T.xt[:, PAD:], T.x[:]).then_inc(S.dx, 16)
     Y.dma_start(T.w1t[:], T.w1[:]).then_inc(S.dw1, 16)
-    for dst, src, sem in ((T.lr1, T.src1, S.dr1), (T.ls2, T.snd2, S.ds2)):
-        for q in range(8):
-            Y.dma_start(dst[16 * q:16 * q + 16, :], src[:, :]).then_inc(sem, 16)
+    n = 0
+    for u in range(4):
+        Y.dma_start(T.lsrc[4 * u:4 * u + 4, 4 - u:260 - u], T.src1[:, :]).then_inc(S.dl, 16)
+        Y.dma_start(T.lsrc[4 * u:4 * u + 4, 260 - u:388 - u], T.src2[:, :]).then_inc(S.dl, 16)
+        n += 2
+    for p, r, w in runs(order):
+        Y.dma_start(T.ls2[0:16, 2 * p:2 * (p + w)], T.snd2[:, 2 * r:2 * (r + w)]).then_inc(S.dl, 16)
+        n += 1
+    nlists = 16 * n
     Y.dma_start(T.w2t[:], T.w2[:]).then_inc(S.dw2, 16)
-    for q in range(8):
-        Y.dma_start(T.lr2[16 * q:16 * q + 16, :], T.src2[:, :]).then_inc(S.dr2, 16)
+    Y.wait_ge(S.lo, 2)
+    for q in range(1, 8):
+        Y.dma_start(T.ol[16 * q:16 * q + 16, 0:OEND], T.ol[0:16, 0:OEND]).then_inc(S.dr, 16)
 
+    V.memset(T.xt[:, 0:PAD], 0.0).then_inc(S.mp, 1)
+    V.memset(T.m1[:], 1.0).then_inc(S.mk, 1)
     for t in range(4):
         a = t * WP + NT + rank * C1
         V.memset(T.wz[:, a:a + C1], 0.0).then_inc(S.mz, 1)
     V.memset(T.uz[:, NT + rank * C2:NT + rank * C2 + C2], 0.0).then_inc(S.mz, 1)
     V.memset(T.hg[:, 4 * 7 * C2:1024], 0.0).then_inc(S.mz, 1)
-    V.memset(T.m1[:], 1.0).then_inc(S.mk, 1)
-    V.memset(T.m2[:], BIG).then_inc(S.mk, 1)
-    V.wait_ge(S.mk, 2)
-    V.memset(T.m1[:, 0:4 * NT:4], 0.0).then_inc(S.ml, 1)
-    V.memset(T.m2[:, 0:2 * TG:4], -BIG).then_inc(S.ml, 1)
+    V.wait_ge(S.mk, 1)
+    V.memset(T.m1[:, 0:3 * NT:3], 0.0).then_inc(S.ml, 1)
 
-    V.wait_ge(S.ds1, 128)
-    V.tensor_scalar(T.of0[:], T.ls1[:], 4, 0, mult, mx).then_inc(S.of0, 1)
-    V.wait_ge(S.of0, 1)
-    for t in (1, 2, 3):
-        V.tensor_scalar(T["of%d" % t][:], T.of0[:], t, None, add).then_inc(S["of%d" % t], 1)
+    V.wait_ge(S.ds1, 32)
+    for q in (1, 2, 3):
+        V.tensor_copy(T.ls1[32 * q:32 * q + 32, :], T.ls1[0:32, :]).then_inc(S.lq, 1)
+    V.wait_ge(S.lq, 3)
+    for t in range(4):
+        V.tensor_scalar(T["of%d" % t][:], T.ls1[:], 4, PAD + t, mult, add).then_inc(S["of%d" % t], 1)
 
-    def pick(eng, pos, t, sem):
-        r = order[pos]
-        out = T.xg[:, 4 * C1 * pos + t:4 * C1 * (pos + 1):4]
-        win = T.xt[:, :].indirect(T["of%d" % t][:, 10 * r:10 * r + 10])
-        if eng is V:
-            V.tensor_copy(out, win).then_inc(sem, 1)
-        else:
-            A.activation(out, win, COPY).then_inc(sem, 1)
-
-    A.wait_ge(S.dx, 16)
-    A.wait_ge(S.of0, 1)
-    A.wait_ge(S.of1, 1)
-    V.wait_ge(S.dx, 16)
-    for t in (1, 2, 3):
-        V.wait_ge(S["of%d" % t], 1)
-    for c, chunk in enumerate(CHUNKS):
-        sem = S["xg%d" % c]
-        if c == 1:
-            A.wait_ge(S.of2, 1)
-        for j, t in SCALAR[c]:
-            pick(A, chunk[j], t, sem)
-        for j in range(len(chunk)):
-            for t in range(4):
-                if (j, t) not in SCALAR[c]:
-                    pick(V, chunk[j], t, sem)
-        V.wait_ge(sem, 4 * len(chunk))
-        a, b = C1 * chunk[0], C1 * (chunk[-1] + 1)
-        V.quantize_mx(T.xgq[:, a:b], T.xgs[:, a:b], T.xg[:, 4 * a:4 * b]).then_inc(S["xq%d" % c], 1)
-
-    V.quantize_mx(T.xq[:], T.xs[:], T.xt[:]).then_inc(S.xo, 1)
-    V.wait_ge(S.dw1, 16)
-    V.quantize_mx(T.w1q[:], T.w1s[:], T.w1t[:]).then_inc(S.w1r, 1)
-    V.wait_ge(S.dr1, 128)
-    V.tensor_copy(T.or1[:], T.lr1[:]).then_inc(S.cr1, 1)
-    V.wait_ge(S.ds2, 128)
-    V.tensor_scalar(T.ti2[:], T.ls2[:], 4, 3, mult, add).then_inc(S.ct2, 1)
-    V.wait_ge(S.ct2, 1)
+    for e in (A, V):
+        e.wait_ge(S.mp, 1)
+        e.wait_ge(S.dx, 16)
     for pos, r in enumerate(order):
-        V.tensor_scalar(T.os2[:, 2 * pos:2 * pos + 2], T.ti2[:, 2 * r:2 * r + 2], 0, None, mx).then_inc(S.cs2, 1)
-    V.wait_ge(S.dw2, 16)
-    V.quantize_mx(T.w2q[:], T.w2s[:], T.w2t[:]).then_inc(S.w2r, 1)
-    V.wait_ge(S.dr2, 128)
-    V.tensor_copy(T.or2[:], T.lr2[:]).then_inc(S.cr2, 1)
+        for t in range(4):
+            eng, name = (A, "A") if t < 4 - VECTOR_GATHERS[pos] else (V, "V")
+            need(eng, name, "of%d" % t, 1)
+            gather(eng, T.xg[:, 4 * C1 * pos + t:4 * C1 * (pos + 1):4],
+                   T.xt[:, :].indirect(T["of%d" % t][:, 10 * r:10 * r + 10]), "xg%d" % pos)
+        call = [c for c in CODE_CALLS if pos in c][0]
+        if pos == 3:
+            V.wait_ge(S.dl, nlists)
+            V.tensor_copy(T.ol[0:16, O1E:OS2], T.lsrc[0:16, 4:388:4]).then_inc(S.lo, 1)
+            V.tensor_copy(T.ol[0:16, OS2:OEND], T.ls2[0:16, 0:14]).then_inc(S.lo, 1)
+        if pos == 5:
+            V.quantize_mx(T.xq[:], T.xs[:], T.xt[:, PAD:]).then_inc(S.xo, 1)
+        if pos == call[-1]:
+            for p in call:
+                V.wait_ge(S["xg%d" % p], 4)
+            a, b = C1 * call[0], C1 * (pos + 1)
+            V.quantize_mx(T.xgq[:, a:b], T.xgs[:, a:b], T.xg[:, 4 * a:4 * b]).then_inc(S["xq%d" % pos], 1)
 
-    def rankof(way, p):
+    V.wait_ge(S.dw1, 16)
+    V.quantize_mx(T.w1q[:, 0:256], T.w1s[:, 0:256], T.w1t[:, 0:1024]).then_inc(S.w1a, 1)
+    V.quantize_mx(T.w1q[:, 256:512], T.w1s[:, 256:512], T.w1t[:, 1024:2048]).then_inc(S.w1b, 1)
+
+    def sender(pos):
         for s in range(N):
             if s != rank:
                 rl, di, _, _ = plan(s, T, topo)
-                if (rl if way == "r" else di)[p] == rank:
+                if (rl + di)[pos] == rank:
                     return s
 
-    srcs = [rankof(w, p) for w, p in (("r", 0), ("r", 1), ("d", 0), ("r", 2), ("r", 3), ("d", 1), ("d", 2))]
-    P.wait_ge(S.w1r, 1)
-    for k in range(8):
+    freed = [0, 0]
+    for k in range(1 + len(EXPECTED)):
         if k == 0:
             P.wait_ge(S.xo, 1)
-            n, base, mq, ms = NT, 0, T.xq[:], T.xs[:]
+            n, parts, mq, ms = NT, [(0, NT)], T.xq[:], T.xs[:]
+            planes, scalar = (0, 1, 2, 3), (0, 1, 2)
         else:
-            s = srcs[k - 1]
-            P.wait_ge(S["arr1_%d" % s], landed(1, s, rank, T, topo))
-            a = C1 * place(s, rank)
-            n, base, mq, ms = C1, NT + C1 * s, T.aq1[:, a:a + C1], T.as1[:, a:a + C1]
-        if k >= 2:
-            P.wait_ge(S["fr%d" % (k - 2)], 4)
-        for i in (0, 2, 1, 3):
+            group = EXPECTED[k - 1]
+            for pos in group:
+                P.wait_ge(S["arr1_%d" % sender(pos)], landed(1, sender(pos), rank, T, topo))
+            a, n = C1 * place1(group[0]), C1 * len(group)
+            parts, mq, ms = [(NT + C1 * sender(pos), C1) for pos in group], T.aq1[:, a:a + n], T.as1[:, a:a + n]
+            planes, scalar = ((0, 2, 1, 3), (0, 1)) if k < len(EXPECTED) else ((0, 1, 2, 3), (0,))
+        for i in planes:
+            need(P, "P", "w1a" if i < 2 else "w1b", 1)
             bank = 512 * (4 * (k % 2) + i)
-            done = S["mm%d_%d" % (k, i)]
+            done, free = "mm%d_%d" % (i, k % 2), "fr%d_%d" % (i, k % 2)
+            if k >= 2:
+                P.wait_ge(S[free], freed[k % 2])
             P.matmul_mx(T.ps[:, bank:bank + n], T.w1q[:, 128 * i:128 * i + 128], T.w1s[:, 128 * i:128 * i + 128],
-                        mq, ms, True, True).then_inc(done, 1)
-            out, res = T.wz[:, WP * i + base:WP * i + base + n], T.ps[:, bank:bank + n]
-            if i < 2:
-                V.wait_ge(done, 1)
-                V.tensor_scalar(out, res, 0.05, 0.0, mult, mx).then_inc(S["fr%d" % k], 1)
-            else:
-                A.wait_ge(done, 1)
-                A.activation(out, res, RELU, scale=0.05).then_inc(S["fr%d" % k], 1)
+                        mq, ms, True, True).then_inc(S[done], 1)
+            (A if i in scalar else V).wait_ge(S[done], k // 2 + 1)
+            for j, (base, w) in enumerate(parts):
+                out, res = T.wz[:, WP * i + base:WP * i + base + w], T.ps[:, bank + w * j:bank + w * j + w]
+                if i in scalar:
+                    A.activation(out, res, RELU, scale=0.05).then_inc(S[free], 1)
+                else:
+                    V.tensor_scalar(out, res, 0.05, 0.0, mult, mx).then_inc(S[free], 1)
+        freed[k % 2] += len(parts)
 
     for e in (V, A):
         e.wait_ge(S.mz, 6)
-        e.wait_ge(S.cr1, 1)
-        e.wait_ge(S.fr6, 4)
-        e.wait_ge(S.fr7, 4)
-    V.wait_ge(S.ml, 2)
-    V.wait_ge(S.cs2, 7)
+        e.wait_ge(S.dr, 112)
+        e.wait_ge(S.lo, 2)
+    V.wait_ge(S.ml, 1)
 
-    def sources(eng, t, h, sem):
-        out = T.gt[:, 1024 * t + 512 * h:1024 * t + 512 * h + 512]
-        win = T.wz[:, WP * t:WP * (t + 1)].indirect(T.or1[:, 32 * h:32 * h + 32])
-        if eng is V:
-            V.tensor_copy(out, win).then_inc(sem, 1)
-        else:
-            A.activation(out, win, COPY).then_inc(sem, 1)
+    def plane(eng, name, t):
+        for b in range(2):
+            need(eng, name, "fr%d_%d" % (t, b), freed[b])
+        return T.wz[:, WP * t:WP * (t + 1)]
 
-    def scan(t, a, b):
-        o = 1024 * t
-        V.tensor_tensor_scan(T.sc[:, o + a:o + b], T.m1[:, a:b], T.gt[:, o + a:o + b], 0.0, mult, mx).then_inc(S["sc%d" % t], 1)
+    def step(t, e):
+        return T.mx[:, NT * (4 * t + e):NT * (4 * t + e + 1)]
 
-    def chosen(t, a, b, sem):
-        V.tensor_copy(T.hg[:, 4 * a + t:4 * b:4],
-                      T.sc[:, 1024 * t:1024 * t + 1024].indirect(T.os2[:, a // 16:b // 16])).then_inc(sem, 1)
+    def first(t):
+        gather(A, step(t, 0), plane(A, "A", t).indirect(T.ol[:, O1E:O1E + 16]), "f%d_0" % t)
 
-    sources(A, 0, 0, S.gh0)
-    sources(A, 1, 0, S.gh1)
-    sources(A, 2, 0, S.gh2)
-    sources(A, 2, 1, S.gh2)
-    sources(A, 3, 0, S.gh3a)
-    sources(A, 3, 1, S.gh3b)
+    def more(t, e):
+        win = plane(V, "V", t).indirect(T.ol[:, O1E + 16 * e:O1E + 16 * e + 16])
+        o = 3 * NT * (t - 2)
+        V.wait_ge(S["f%d_%d" % (t, e - 1)], 1)
+        V.tensor_tensor(step(t, e), win, step(t, e - 1) if t < 2 else T.sc[:, o + 2:o + 3 * NT:3],
+                        mx).then_inc(S["f%d_%d" % (t, e)], 1)
 
-    sources(V, 0, 1, S.gh0)
-    V.wait_ge(S.gh0, 2)
-    scan(0, 0, 1024)
-    sources(V, 1, 1, S.gh1)
-    V.wait_ge(S.gh1, 2)
-    scan(1, 0, 1024)
-    V.wait_ge(S.sc0, 1)
-    chosen(0, 0, 7 * C2, S.sgr)
-    V.wait_ge(S.sc1, 1)
-    chosen(1, 0, 7 * C2, S.sgr)
-    V.wait_ge(S.gh2, 2)
-    scan(2, 0, 1024)
-    V.wait_ge(S.sc2, 1)
-    chosen(2, 0, 7 * C2, S.sgr)
-    V.wait_ge(S.gh3a, 1)
-    scan(3, 0, 512)
-    V.wait_ge(S.gh3b, 1)
-    scan(3, 512, 1024)
-    V.wait_ge(S.sc3, 2)
-    chosen(3, 0, 128, S.sgr)
-    V.wait_ge(S.sgr, 4)
+    def three(t):
+        o = 3 * NT * (t - 2)
+        for e in range(3):
+            gather(A, T.gt[:, o + e:o + 3 * NT:3], plane(A, "A", t).indirect(T.ol[:, O1E + 16 * e:O1E + 16 * e + 16]),
+                   "g%d" % t)
+
+    def scan(t):
+        o = 3 * NT * (t - 2)
+        V.wait_ge(S["g%d" % t], 3)
+        V.tensor_tensor_scan(T.sc[:, o:o + 3 * NT], T.m1[:], T.gt[:, o:o + 3 * NT], 0.0, mult, mx).then_inc(S["f%d_2" % t], 1)
+
+    def chosen(eng, name, t, a, b, sem):
+        need(eng, name, "f%d_3" % t, 1)
+        gather(eng, T.hg[:, 4 * a + t:4 * b:4], step(t, 3).indirect(T.ol[:, OS2 + a // 16:OS2 + b // 16]), sem)
+
+    first(0)
+    first(1)
+    three(2)
+    three(3)
+    for t in (0, 1, 2):
+        chosen(A, "A", t, 0, 7 * C2, "cf")
+    chosen(A, "A", 3, 128, 7 * C2, "cd")
+
+    for e in (1, 2, 3):
+        more(0, e)
+        more(1, e)
+    for t in (2, 3):
+        scan(t)
+        more(t, 3)
+    chosen(V, "V", 3, 0, 128, "cf")
+    V.wait_ge(S.cf, 4)
     V.quantize_mx(T.hgq[:, 0:128], T.hgs[:, 0:128], T.hg[:, 0:512]).then_inc(S.hqr, 1)
-    chosen(3, 128, 7 * C2, S.sgd)
-    V.wait_ge(S.sgd, 1)
+    V.wait_ge(S.cd, 1)
     V.quantize_mx(T.hgq[:, 128:256], T.hgs[:, 128:256], T.hg[:, 512:1024]).then_inc(S.hqd, 1)
 
-    for t in range(4):
-        A.wait_ge(S["sc%d" % t], 2 if t == 3 else 1)
-        A.activation(T.ht[:, t:4 * NT:4], T.sc[:, 1024 * t + 3:1024 * t + 1024:4], COPY).then_inc(S.hc, 1)
+    A.activation(T.ht[:, 0:4 * NT:4], step(0, 3), COPY).then_inc(S.hc, 1)
+    for t in (1, 2, 3):
+        need(V, "V", "f%d_3" % t, 1)
+        V.tensor_copy(T.ht[:, t:4 * NT:4], step(t, 3)).then_inc(S.hc, 1)
+    V.wait_ge(S.dw2, 16)
+    V.quantize_mx(T.w2q[:], T.w2s[:], T.w2t[:]).then_inc(S.w2r, 1)
     V.wait_ge(S.hc, 4)
     V.quantize_mx(T.htq[:], T.hts[:], T.ht[:]).then_inc(S.hor, 1)
 
+    for i in range(4):
+        for b in range(2):
+            P.wait_ge(S["fr%d_%d" % (i, b)], freed[b])
     P.wait_ge(S.w2r, 1)
     P.wait_ge(S.hor, 1)
     P.matmul_mx(T.ps[:, 0:NT], T.w2q[:], T.w2s[:], T.htq[:], T.hts[:], True, True).then_inc(S.m2o, 1)
@@ -300,8 +335,8 @@ def rank_program(g, core, T, topo):
             P.wait_ge(S["arr2_%d" % s], landed(2, s, rank, T, topo))
     P.matmul_mx(T.ps[:, 2048:2176], T.w2q[:], T.w2s[:], T.aq2[:, 0:128], T.as2[:, 0:128], True, True).then_inc(S.m2a, 1)
     P.matmul_mx(T.ps[:, 2560:2688], T.w2q[:], T.w2s[:], T.aq2[:, 96:224], T.as2[:, 96:224], True, True).then_inc(S.m2b, 1)
-    V.wait_ge(S.m2a, 1)
-    A.wait_ge(S.m2b, 1)
+    A.wait_ge(S.m2a, 1)
+    V.wait_ge(S.m2b, 1)
     done, hole = 1, C2 * rank
     for a, b, bank in ((0, 112, 2048), (112, 224, 2560 - 96)):
         for lo, hi in ((a, min(b, hole)), (max(a, hole), b)):
@@ -309,22 +344,29 @@ def rank_program(g, core, T, topo):
                 o = NT + lo + (C2 if lo >= hole else 0)
                 out, res = T.uz[:, o:o + hi - lo], T.ps[:, bank + lo:bank + hi]
                 if a == 0:
-                    V.tensor_copy(out, res).then_inc(S.ud, 1)
-                else:
                     A.activation(out, res, COPY).then_inc(S.ud, 1)
+                else:
+                    V.tensor_copy(out, res).then_inc(S.ud, 1)
                 done += 1
 
-    V.wait_ge(S.cr2, 1)
-    A.wait_ge(S.cr2, 1)
     V.wait_ge(S.ud, done)
     A.wait_ge(S.ud, done)
-    V.tensor_copy(T.gu[:, 0:256], T.uz[:, :].indirect(T.or2[:, 0:16])).then_inc(S.g2a, 1)
-    A.activation(T.gu[:, 256:512], T.uz[:, :].indirect(T.or2[:, 16:32]), COPY).then_inc(S.g2b, 1)
-    for h, sem in ((0, S.g2a), (256, S.g2b)):
-        V.wait_ge(sem, 1)
-        V.tensor_tensor_scan(T.su[:, h:h + 256], T.m2[:], T.gu[:, h:h + 256], 0.0, AluOpType.min, mx).then_inc(S.sca, 1)
-    V.wait_ge(S.sca, 2)
-    V.tensor_copy(T.yt[:], T.su[:, 3:4 * TG:4]).then_inc(S.yc, 1)
+
+    def src(e):
+        return T.uz[:, :].indirect(T.ol[:, O2E + 8 * e:O2E + 8 * e + 8])
+
+    def part(e):
+        return T.gu[:, TG * e:TG * e + TG]
+
+    gather(A, part(0), src(0), "u0")
+    gather(V, part(1), src(1), "u1")
+    V.wait_ge(S.u0, 1)
+    V.tensor_tensor(part(2), src(2), part(0), mx).then_inc(S.u2, 1)
+    V.wait_ge(S.u1, 1)
+    V.tensor_tensor(part(3), src(3), part(1), mx).then_inc(S.u3, 1)
+    V.wait_ge(S.u2, 1)
+    V.wait_ge(S.u3, 1)
+    V.tensor_tensor(T.yt[:], part(2), part(3), mx).then_inc(S.yc, 1)
     Y.wait_ge(S.yc, 1)
     Y.dma_start(T.y[:], T.yt[:]).then_inc(S.ys, 16)
     Y.wait_ge(S.ys, 16)
@@ -340,38 +382,39 @@ def rank_program(g, core, T, topo):
             sent[0] += len(es)
         g.remote_dma_fused(ts, local_sem=S.sent)
 
-    for c, chunk in enumerate(CHUNKS):
-        g.wait_ge(S["xq%d" % c], 1)
-        codes, planes = [], []
-        for j, pos in enumerate(chunk):
-            a = C1 * pos
-            r = order[pos]
-            d = help1[pos] if pos < 4 else T.cores[r]
-            es = topo.engines(core, d)
-            w = len(es) // len(chunk)
-            es = es[w * j:w * j + w]
-            sq, ss = b8(T.xgq[:, a:a + C1]), T.xgs[:, a:a + C1]
-            if pos < 4:
-                codes.append((d, es, sq, b8(T.hq1[:, :]), S.rc1))
-                planes.append((d, es, ss, T.hs1[:, :], S.rs1))
-            else:
-                o = C1 * place(rank, r)
-                sem = S["arr1_%d" % rank]
-                codes.append((d, es, sq, b8(T.aq1[:, o:o + C1]), sem))
-                planes.append((d, es, ss, T.as1[:, o:o + C1], sem))
-        fused(codes)
-        fused(planes)
+    def piece(pos, code):
+        a, r = C1 * pos, order[pos]
+        if pos < 4:
+            d = help1[0 if code else 1][pos]
+            j = help1[0 if code else 1][:pos].count(d)
+            o, sem, dq, ds = C1 * j, S[("rc1" if code else "rs1") + "ab"[j]], T.hq1, T.hs1
+        else:
+            d = T.cores[r]
+            o, sem, dq, ds = C1 * place1(pos), S["arr1_%d" % rank], T.aq1, T.as1
+        es = share(topo.engines(core, d), CODE_CALLS if code else PLANE_CALLS, pos)
+        if code:
+            return d, es, b8(T.xgq[:, a:a + C1]), b8(dq[:, o:o + C1]), sem
+        return d, es, T.xgs[:, a:a + C1], ds[:, o:o + C1], sem
+
+    for last in [c[-1] for c in CODE_CALLS]:
+        g.wait_ge(S["xq%d" % last], 1)
+        for code, calls in ((True, CODE_CALLS), (False, PLANE_CALLS)):
+            for call in calls:
+                if call[-1] == last:
+                    fused([piece(pos, code) for pos in call])
 
     g.wait_ge(S.hqr, 1)
-    codes, planes = [], []
-    for j, d in enumerate(help2):
-        es = topo.engines(core, d)
-        es = es[len(es) // 2 * j:len(es) // 2 * (j + 1)]
-        a = 2 * C2 * j
-        codes.append((d, es, b8(T.hgq[:, a:a + 2 * C2]), b8(T.hq2[:, :]), S.rc2))
-        planes.append((d, es, T.hgs[:, a:a + 2 * C2], T.hs2[:, :], S.rs2))
-    fused(codes)
-    fused(planes)
+    for code in (True, False):
+        parts = []
+        for j, d in enumerate(help2[0 if code else 1]):
+            es = topo.engines(core, d)
+            es = es[len(es) // 2 * j:len(es) // 2 * (j + 1)]
+            a = 2 * C2 * j
+            if code:
+                parts.append((d, es, b8(T.hgq[:, a:a + 2 * C2]), b8(T.hq2[:, :]), S.r2))
+            else:
+                parts.append((d, es, T.hgs[:, a:a + 2 * C2], T.hs2[:, :], S.r2s))
+        fused(parts)
     g.wait_ge(S.hqd, 1)
     codes, planes = [], []
     for j, r in enumerate(direct):
@@ -390,35 +433,40 @@ def helper(g, core, s, T, topo):
     relayed, _, help1, help2 = plan(s, T, topo)
     S = T.sem
     me = T.cores[s]
+    mine = topo.engines(me, core)
     sent = 0
-    if core in help1:
-        j = help1.index(core)
-        w = len(topo.engines(me, core)) // 2
-        r = relayed[j]
-        d = T.cores[r]
-        o = C1 * place(s, r)
-        rid, pid = topo.addr(d, core)
-        for sem, out, src in ((S.rc1, b8(T.aq1[:, o:o + C1]), b8(T.hq1[:, :])), (S.rs1, T.as1[:, o:o + C1], T.hs1[:, :])):
-            g.wait_ge(sem, w)
+    for pos in range(4):
+        for code in (True, False):
+            by = help1[0 if code else 1]
+            if by[pos] != core:
+                continue
+            j = by[:pos].count(core)
+            d = T.cores[relayed[pos]]
+            o, a = C1 * place1(pos), C1 * j
+            rid, pid = topo.addr(d, core)
+            if code:
+                sem, calls, out, src = "rc1", CODE_CALLS, b8(T.aq1[:, o:o + C1]), b8(T.hq1[:, a:a + C1])
+            else:
+                sem, calls, out, src = "rs1", PLANE_CALLS, T.as1[:, o:o + C1], T.hs1[:, a:a + C1]
+            g.wait_ge(S[sem + "ab"[j]], len(share(mine, calls, pos)))
             g.remote_dma(out, src, S["arr1_%d" % s], S.sent, pid, rid, topo.mask(core, d))
             sent += len(topo.engines(core, d))
-    if core in help2:
-        j = help2.index(core)
-        w = len(topo.engines(me, core)) // 2
-        two = relayed[2 * j:2 * j + 2]
-        for sem, code in ((S.rc2, True), (S.rs2, False)):
-            g.wait_ge(sem, w)
-            ts = []
-            for i, r in enumerate(two):
-                d = T.cores[r]
-                es = topo.engines(core, d)[4 * i:4 * i + 4]
-                o, a = C2 * place(s, r), C2 * i
-                src = b8(T.hq2[:, a:a + C2]) if code else T.hs2[:, a:a + C2]
-                dst = b8(T.aq2[:, o:o + C2]) if code else T.as2[:, o:o + C2]
-                rid, pid = topo.addr(d, core)
-                ts.append(RemoteDMATransfer(dst_ids=[DstId(rid=rid, pnc=pid)], dma_engine_mask=bits(es),
-                                            remote_sem=S["arr2_%d" % s], src=src, dst=dst))
-                sent += len(es)
-            g.remote_dma_fused(ts, local_sem=S.sent)
+    for code in (True, False):
+        if core not in help2[0 if code else 1]:
+            continue
+        j = help2[0 if code else 1].index(core)
+        g.wait_ge(S.r2 if code else S.r2s, len(mine) // 2)
+        ts = []
+        for i, r in enumerate(relayed[2 * j:2 * j + 2]):
+            d = T.cores[r]
+            es = topo.engines(core, d)[4 * i:4 * i + 4]
+            o, a = C2 * place(s, r), C2 * i
+            src = b8(T.hq2[:, a:a + C2]) if code else T.hs2[:, a:a + C2]
+            dst = b8(T.aq2[:, o:o + C2]) if code else T.as2[:, o:o + C2]
+            rid, pid = topo.addr(d, core)
+            ts.append(RemoteDMATransfer(dst_ids=[DstId(rid=rid, pnc=pid)], dma_engine_mask=bits(es),
+                                        remote_sem=S["arr2_%d" % s], src=src, dst=dst))
+            sent += len(es)
+        g.remote_dma_fused(ts, local_sem=S.sent)
     if sent:
         g.wait_ge(S.sent, sent)

@@ -5,7 +5,8 @@ N, NT, TG, C1, C2 = 8, 256, 128, 160, 32
 WP = NT + N * C1
 UP = NT + N * C2
 PAD = 16
-O1E, O2E, OS2, OEND = 0, 64, 96, 110
+SP = 2 * PAD + 4 * NT
+O1E, O2E, O1N, OS2, OS4, OEND = 0, 64, 96, 160, 174, 188
 
 SCRATCH = {
     "xt": ("sbuf", [128, PAD + 4 * NT], "bfloat16"),
@@ -13,8 +14,8 @@ SCRATCH = {
     "w2t": ("sbuf", [128, 512], "bfloat16"),
     "ls1": ("sbuf", [128, 80], "int32"),
     "lsrc": ("sbuf", [128, 388], "int32"),
-    "ls2": ("sbuf", [128, 16], "int32"),
-    "ol": ("sbuf", [128, 112], "uint16"),
+    "lmix": ("sbuf", [128, 80], "int32"),
+    "ol": ("sbuf", [128, 192], "uint16"),
     "of0": ("sbuf", [128, 80], "uint16"),
     "of1": ("sbuf", [128, 80], "uint16"),
     "of2": ("sbuf", [128, 80], "uint16"),
@@ -37,10 +38,10 @@ SCRATCH = {
     "hq2": ("sbuf", [128, 2 * C2], "float8_e4m3fn_x4"),
     "hs2": ("sbuf", [128, 2 * C2], "uint8"),
     "wz": ("sbuf", [128, 4 * WP], "bfloat16"),
-    "mx": ("sbuf", [128, 16 * NT], "bfloat16"),
-    "gt": ("sbuf", [128, 2 * 3 * NT], "bfloat16"),
-    "sc": ("sbuf", [128, 2 * 3 * NT], "bfloat16"),
-    "m1": ("sbuf", [128, 3 * NT], "bfloat16"),
+    "mx": ("sbuf", [128, 8 * NT], "bfloat16"),
+    "gt": ("sbuf", [128, 2 * 4 * NT], "bfloat16"),
+    "sc": ("sbuf", [128, 2 * SP], "bfloat16"),
+    "m1": ("sbuf", [128, 2 * NT], "bfloat16"),
     "hg": ("sbuf", [128, 4 * 256], "bfloat16"),
     "hgq": ("sbuf", [128, 256], "float8_e4m3fn_x4"),
     "hgs": ("sbuf", [128, 256], "uint8"),
@@ -54,17 +55,18 @@ SCRATCH = {
 }
 SEMAPHORES = (["dx", "dw1", "dw2", "ds1", "dl", "dr", "mz", "mp", "mk", "ml", "xo", "w1a", "w1b", "w2r", "lo",
                "cf", "cd", "hqr", "hqd", "hc", "hor", "m2o", "m2a", "m2b", "ud", "yc", "ys",
-               "sent", "rc1a", "rs1a", "rc1b", "rs1b", "r2", "r2s", "lq", "g2", "g3"]
+               "sent", "rc1a", "rs1a", "rc1b", "rs1b", "r2", "r2s", "lq", "g2", "g3a", "g3b"]
               + ["of%d" % t for t in range(4)] + ["xg%d" % c for c in range(7)] + ["xq%d" % c for c in range(7)]
               + ["mm%d_%d" % (i, b) for i in range(4) for b in range(2)]
               + ["fr%d_%d" % (i, b) for i in range(4) for b in range(2)]
               + ["f%d_%d" % (t, e) for t in range(4) for e in range(4) if t < 2 or e > 1] + ["u%d" % e for e in range(4)]
               + ["arr%d_%d" % (l, s) for l in (1, 2) for s in range(N)])
 
-VECTOR_GATHERS = (2, 2, 2, 1, 2, 1, 2)
-CODE_CALLS = ((0, 1), (2, 3), (4,), (5,), (6,))
+SEQUENCE = (0, 1, 4, 2, 3, 5, 6)
+VECTOR_GATHERS = (2, 2, 2, 1, 1, 1, 2)
+CODE_CALLS = ((0,), (1,), (2,), (3,), (4,), (5,), (6,))
 PLANE_CALLS = ((0, 1), (2, 3), (4,), (5,), (6,))
-EXPECTED = ((0,), (1,), (4,), (2,), (5,), (3,), (6,))
+EXPECTED = ((4,), (0,), (1,), (2,), (5,), (3,), (6,))
 
 
 def plan(s, T, topo):
@@ -156,56 +158,62 @@ def rank_program(g, core, T, topo):
         else:
             A.activation(out, win, COPY).then_inc(S[sem], 1)
 
-    for q, e in enumerate((A, Y)):
+    for q, e in enumerate((A, Y, A, Y)):
         e.dma_start(T.ls1[16 * q:16 * q + 16, :], T.snd1[:, :]).then_inc(S.ds1, 16)
     Y.dma_start(T.xt[:, PAD:], T.x[:]).then_inc(S.dx, 16)
     Y.dma_start(T.w1t[:], T.w1[:]).then_inc(S.dw1, 16)
-    n = 0
+    Y.dma_start(T.lmix[0:16, 0:64], T.src1[:, :]).then_inc(S.dl, 16)
+    n = 1
     for u in range(4):
         Y.dma_start(T.lsrc[4 * u:4 * u + 4, 4 - u:260 - u], T.src1[:, :]).then_inc(S.dl, 16)
         Y.dma_start(T.lsrc[4 * u:4 * u + 4, 260 - u:388 - u], T.src2[:, :]).then_inc(S.dl, 16)
         n += 2
     for p, r, w in runs(order):
-        Y.dma_start(T.ls2[0:16, 2 * p:2 * (p + w)], T.snd2[:, 2 * r:2 * (r + w)]).then_inc(S.dl, 16)
+        Y.dma_start(T.lmix[0:16, 64 + 2 * p:64 + 2 * (p + w)], T.snd2[:, 2 * r:2 * (r + w)]).then_inc(S.dl, 16)
         n += 1
     nlists = 16 * n
     Y.dma_start(T.w2t[:], T.w2[:]).then_inc(S.dw2, 16)
-    Y.wait_ge(S.lo, 2)
+    Y.wait_ge(S.lo, 3)
     for q in range(1, 8):
         Y.dma_start(T.ol[16 * q:16 * q + 16, 0:OEND], T.ol[0:16, 0:OEND]).then_inc(S.dr, 16)
 
     V.memset(T.xt[:, 0:PAD], 0.0).then_inc(S.mp, 1)
     V.memset(T.m1[:], 1.0).then_inc(S.mk, 1)
+    A.wait_ge(S.ml, 1)
     for t in range(4):
         a = t * WP + NT + rank * C1
-        V.memset(T.wz[:, a:a + C1], 0.0).then_inc(S.mz, 1)
+        A.activation(T.wz[:, a:a + C1], T.m1[:, 0:C1], COPY).then_inc(S.mz, 1)
     V.memset(T.uz[:, NT + rank * C2:NT + rank * C2 + C2], 0.0).then_inc(S.mz, 1)
     V.memset(T.hg[:, 4 * 7 * C2:1024], 0.0).then_inc(S.mz, 1)
     V.wait_ge(S.mk, 1)
-    V.memset(T.m1[:, 0:3 * NT:3], 0.0).then_inc(S.ml, 1)
+    V.memset(T.m1[:, 0:2 * NT:4], 0.0).then_inc(S.ml, 1)
 
-    V.wait_ge(S.ds1, 32)
-    for q in (1, 2, 3):
-        V.tensor_copy(T.ls1[32 * q:32 * q + 32, :], T.ls1[0:32, :]).then_inc(S.lq, 1)
-    V.wait_ge(S.lq, 3)
+    V.wait_ge(S.ds1, 64)
+    V.tensor_copy(T.ls1[64:128, :], T.ls1[0:64, :]).then_inc(S.lq, 1)
+    V.wait_ge(S.lq, 1)
     for t in range(4):
         V.tensor_scalar(T["of%d" % t][:], T.ls1[:], 4, PAD + t, mult, add).then_inc(S["of%d" % t], 1)
 
     for e in (A, V):
         e.wait_ge(S.mp, 1)
         e.wait_ge(S.dx, 16)
-    for pos, r in enumerate(order):
+    for turn, pos in enumerate(SEQUENCE):
+        r = order[pos]
         for t in range(4):
-            eng, name = (A, "A") if t < 4 - VECTOR_GATHERS[pos] else (V, "V")
+            eng, name = (A, "A") if t < 4 - VECTOR_GATHERS[turn] else (V, "V")
             need(eng, name, "of%d" % t, 1)
             gather(eng, T.xg[:, 4 * C1 * pos + t:4 * C1 * (pos + 1):4],
                    T.xt[:, :].indirect(T["of%d" % t][:, 10 * r:10 * r + 10]), "xg%d" % pos)
         call = [c for c in CODE_CALLS if pos in c][0]
-        if pos == 3:
+        if turn == 3:
             V.wait_ge(S.dl, nlists)
-            V.tensor_copy(T.ol[0:16, O1E:OS2], T.lsrc[0:16, 4:388:4]).then_inc(S.lo, 1)
-            V.tensor_copy(T.ol[0:16, OS2:OEND], T.ls2[0:16, 0:14]).then_inc(S.lo, 1)
-        if pos == 5:
+            V.tensor_copy(T.ol[0:16, O1E:O1N], T.lsrc[0:16, 4:388:4]).then_inc(S.lo, 1)
+            V.tensor_copy(T.ol[0:16, O1N:OS4], T.lmix[0:16, 0:78]).then_inc(S.lo, 1)
+            V.tensor_scalar(T.ol[0:16, OS4:OEND], T.lmix[0:16, 64:78], 0, 4, mx, mult).then_inc(S.lo, 1)
+        if turn == 4:
+            V.wait_ge(S.dw1, 16)
+            V.quantize_mx(T.w1q[:, 0:256], T.w1s[:, 0:256], T.w1t[:, 0:1024]).then_inc(S.w1a, 1)
+        if turn == 5:
             V.quantize_mx(T.xq[:], T.xs[:], T.xt[:, PAD:]).then_inc(S.xo, 1)
         if pos == call[-1]:
             for p in call:
@@ -213,8 +221,6 @@ def rank_program(g, core, T, topo):
             a, b = C1 * call[0], C1 * (pos + 1)
             V.quantize_mx(T.xgq[:, a:b], T.xgs[:, a:b], T.xg[:, 4 * a:4 * b]).then_inc(S["xq%d" % pos], 1)
 
-    V.wait_ge(S.dw1, 16)
-    V.quantize_mx(T.w1q[:, 0:256], T.w1s[:, 0:256], T.w1t[:, 0:1024]).then_inc(S.w1a, 1)
     V.quantize_mx(T.w1q[:, 256:512], T.w1s[:, 256:512], T.w1t[:, 1024:2048]).then_inc(S.w1b, 1)
 
     def sender(pos):
@@ -257,7 +263,7 @@ def rank_program(g, core, T, topo):
     for e in (V, A):
         e.wait_ge(S.mz, 6)
         e.wait_ge(S.dr, 112)
-        e.wait_ge(S.lo, 2)
+        e.wait_ge(S.lo, 3)
     V.wait_ge(S.ml, 1)
 
     def plane(eng, name, t):
@@ -266,6 +272,8 @@ def rank_program(g, core, T, topo):
         return T.wz[:, WP * t:WP * (t + 1)]
 
     def step(t, e):
+        if t > 1:
+            return T.sc[:, SP * (t - 2) + PAD:SP * (t - 2) + PAD + 4 * NT:4]
         return T.mx[:, NT * (4 * t + e):NT * (4 * t + e + 1)]
 
     def first(t):
@@ -273,40 +281,42 @@ def rank_program(g, core, T, topo):
 
     def more(t, e):
         win = plane(V, "V", t).indirect(T.ol[:, O1E + 16 * e:O1E + 16 * e + 16])
-        o = 3 * NT * (t - 2)
         V.wait_ge(S["f%d_%d" % (t, e - 1)], 1)
-        V.tensor_tensor(step(t, e), win, step(t, e - 1) if t < 2 else T.sc[:, o + 2:o + 3 * NT:3],
-                        mx).then_inc(S["f%d_%d" % (t, e)], 1)
+        V.tensor_tensor(step(t, e), win, step(t, e - 1), mx).then_inc(S["f%d_%d" % (t, e)], 1)
 
-    def three(t):
-        o = 3 * NT * (t - 2)
-        for e in range(3):
-            gather(A, T.gt[:, o + e:o + 3 * NT:3], plane(A, "A", t).indirect(T.ol[:, O1E + 16 * e:O1E + 16 * e + 16]),
-                   "g%d" % t)
+    def four(t, a, b, sem):
+        o = 4 * NT * (t - 2)
+        gather(A, T.gt[:, o + a:o + b], plane(A, "A", t).indirect(T.ol[:, O1N + a // 16:O1N + b // 16]), sem)
 
-    def scan(t):
-        o = 3 * NT * (t - 2)
-        V.wait_ge(S["g%d" % t], 3)
-        V.tensor_tensor_scan(T.sc[:, o:o + 3 * NT], T.m1[:], T.gt[:, o:o + 3 * NT], 0.0, mult, mx).then_inc(S["f%d_2" % t], 1)
+    def scan(t, a, b, sem):
+        o, p = 4 * NT * (t - 2), SP * (t - 2) + PAD - 3
+        need(V, "V", sem, 1)
+        V.tensor_tensor_scan(T.sc[:, p + a:p + b], T.m1[:], T.gt[:, o + a:o + b], 0.0, mult,
+                             mx).then_inc(S["f%d_3" % t], 1)
 
     def chosen(eng, name, t, a, b, sem):
-        need(eng, name, "f%d_3" % t, 1)
-        gather(eng, T.hg[:, 4 * a + t:4 * b:4], step(t, 3).indirect(T.ol[:, OS2 + a // 16:OS2 + b // 16]), sem)
+        need(eng, name, "f%d_3" % t, 2 if t > 1 else 1)
+        o = SP * (t - 2) + PAD
+        win, of = (step(t, 3), OS2) if t < 2 else (T.sc[:, o:o + 4 * NT - 3], OS4)
+        gather(eng, T.hg[:, 4 * a + t:4 * b:4], win.indirect(T.ol[:, of + a // 16:of + b // 16]), sem)
 
     first(0)
     first(1)
-    three(2)
-    three(3)
-    for t in (0, 1, 2):
+    four(2, 0, 1024, "g2")
+    four(3, 0, 512, "g3a")
+    four(3, 512, 1024, "g3b")
+    for t in (0, 1):
         chosen(A, "A", t, 0, 7 * C2, "cf")
     chosen(A, "A", 3, 128, 7 * C2, "cd")
 
     for e in (1, 2, 3):
         more(0, e)
         more(1, e)
-    for t in (2, 3):
-        scan(t)
-        more(t, 3)
+    scan(2, 0, 512, "g2")
+    scan(2, 512, 1024, "g2")
+    scan(3, 0, 512, "g3a")
+    chosen(V, "V", 2, 0, 7 * C2, "cf")
+    scan(3, 512, 1024, "g3b")
     chosen(V, "V", 3, 0, 128, "cf")
     V.wait_ge(S.cf, 4)
     V.quantize_mx(T.hgq[:, 0:128], T.hgs[:, 0:128], T.hg[:, 0:512]).then_inc(S.hqr, 1)
@@ -315,7 +325,7 @@ def rank_program(g, core, T, topo):
 
     A.activation(T.ht[:, 0:4 * NT:4], step(0, 3), COPY).then_inc(S.hc, 1)
     for t in (1, 2, 3):
-        need(V, "V", "f%d_3" % t, 1)
+        need(V, "V", "f%d_3" % t, 2 if t > 1 else 1)
         V.tensor_copy(T.ht[:, t:4 * NT:4], step(t, 3)).then_inc(S.hc, 1)
     V.wait_ge(S.dw2, 16)
     V.quantize_mx(T.w2q[:], T.w2s[:], T.w2t[:]).then_inc(S.w2r, 1)
@@ -396,7 +406,7 @@ def rank_program(g, core, T, topo):
             return d, es, b8(T.xgq[:, a:a + C1]), b8(dq[:, o:o + C1]), sem
         return d, es, T.xgs[:, a:a + C1], ds[:, o:o + C1], sem
 
-    for last in [c[-1] for c in CODE_CALLS]:
+    for last in [p for p in SEQUENCE if p in [c[-1] for c in CODE_CALLS]]:
         g.wait_ge(S["xq%d" % last], 1)
         for code, calls in ((True, CODE_CALLS), (False, PLANE_CALLS)):
             for call in calls:

from concourse.bass import DstId, RemoteDMATransfer
from concourse.mybir import dt, AluOpType, ActivationFunctionType

N, NT, TG, C1, C2 = 8, 256, 128, 160, 32
WP = NT + N * C1
UP = NT + N * C2
PAD = 16
SP = 2 * PAD + 4 * NT
O1E, O2E, O1N, OS2, OS4, OEND = 0, 64, 96, 160, 174, 188

SCRATCH = {
    "xt": ("sbuf", [128, PAD + 4 * NT], "bfloat16"),
    "w1t": ("sbuf", [128, 2048], "bfloat16"),
    "w2t": ("sbuf", [128, 512], "bfloat16"),
    "ls1": ("sbuf", [128, 80], "int32"),
    "lsrc": ("sbuf", [128, 388], "int32"),
    "lmix": ("sbuf", [128, 80], "int32"),
    "ol": ("sbuf", [128, 192], "uint16"),
    "of0": ("sbuf", [128, 80], "uint16"),
    "of1": ("sbuf", [128, 80], "uint16"),
    "of2": ("sbuf", [128, 80], "uint16"),
    "of3": ("sbuf", [128, 80], "uint16"),
    "xg": ("sbuf", [128, 7 * 4 * C1], "bfloat16"),
    "xgq": ("sbuf", [128, 7 * C1], "float8_e4m3fn_x4"),
    "xgs": ("sbuf", [128, 7 * C1], "uint8"),
    "xq": ("sbuf", [128, NT], "float8_e4m3fn_x4"),
    "xs": ("sbuf", [128, NT], "uint8"),
    "w1q": ("sbuf", [128, 512], "float8_e4m3fn_x4"),
    "w1s": ("sbuf", [128, 512], "uint8"),
    "w2q": ("sbuf", [128, 128], "float8_e4m3fn_x4"),
    "w2s": ("sbuf", [128, 128], "uint8"),
    "aq1": ("sbuf", [128, 7 * C1], "float8_e4m3fn_x4"),
    "as1": ("sbuf", [128, 7 * C1], "uint8"),
    "aq2": ("sbuf", [128, 7 * C2], "float8_e4m3fn_x4"),
    "as2": ("sbuf", [128, 7 * C2], "uint8"),
    "hq1": ("sbuf", [128, 2 * C1], "float8_e4m3fn_x4"),
    "hs1": ("sbuf", [128, 2 * C1], "uint8"),
    "hq2": ("sbuf", [128, 2 * C2], "float8_e4m3fn_x4"),
    "hs2": ("sbuf", [128, 2 * C2], "uint8"),
    "wz": ("sbuf", [128, 4 * WP], "bfloat16"),
    "mx": ("sbuf", [128, 8 * NT], "bfloat16"),
    "gt": ("sbuf", [128, 2 * 4 * NT], "bfloat16"),
    "sc": ("sbuf", [128, 2 * SP], "bfloat16"),
    "m1": ("sbuf", [128, 2 * NT], "bfloat16"),
    "hg": ("sbuf", [128, 4 * 256], "bfloat16"),
    "hgq": ("sbuf", [128, 256], "float8_e4m3fn_x4"),
    "hgs": ("sbuf", [128, 256], "uint8"),
    "ht": ("sbuf", [128, 4 * NT], "bfloat16"),
    "htq": ("sbuf", [128, NT], "float8_e4m3fn_x4"),
    "hts": ("sbuf", [128, NT], "uint8"),
    "uz": ("sbuf", [128, UP], "float32"),
    "gu": ("sbuf", [128, 4 * TG], "float32"),
    "yt": ("sbuf", [128, TG], "float32"),
    "ps": ("psum", [128, 4096], "float32"),
}
SEMAPHORES = (["dx", "dw1", "dw2", "ds1", "dl", "dr", "mz", "mp", "mk", "ml", "xo", "w1a", "w1b", "w2r", "lo",
               "cf", "cd", "hqr", "hqd", "hc", "hor", "m2o", "m2a", "m2b", "ud", "yc", "ys",
               "sent", "rc1a", "rs1a", "rc1b", "rs1b", "r2", "r2s", "lq", "g2", "g3a", "g3b"]
              + ["of%d" % t for t in range(4)] + ["xg%d" % c for c in range(7)] + ["xq%d" % c for c in range(7)]
              + ["mm%d_%d" % (i, b) for i in range(4) for b in range(2)]
              + ["fr%d_%d" % (i, b) for i in range(4) for b in range(2)]
              + ["f%d_%d" % (t, e) for t in range(4) for e in range(4) if t < 2 or e > 1] + ["u%d" % e for e in range(4)]
              + ["arr%d_%d" % (l, s) for l in (1, 2) for s in range(N)])

SEQUENCE = (0, 1, 4, 2, 3, 5, 6)
VECTOR_GATHERS = (2, 2, 2, 1, 1, 1, 2)
CODE_CALLS = ((0,), (1,), (2,), (3,), (4,), (5,), (6,))
PLANE_CALLS = ((0, 1), (2, 3), (4,), (5,), (6,))
EXPECTED = ((4,), (0,), (1,), (2,), (5,), (3,), (6,))


def plan(s, T, topo):
    me = T.cores[s]
    near = [r for r in range(N) if r == s or topo.may_write(me, T.cores[r])]
    far = [r for r in range(N) if r not in near]
    i = near.index(s)
    relayed = [far[(i + k) % len(far)] for k in range(len(far))]
    direct = [near[(i + k) % len(near)] for k in range(1, len(near))]
    help_ = [c for c in topo.cores_of(me) if c != me and all(topo.may_write(c, T.cores[r]) for r in far)]
    other = [c for c in help_ if topo.die(c) != topo.die(me)]
    own = [c for c in help_ if topo.die(c) == topo.die(me)]
    return relayed, direct, (2 * other[:2], 2 * own[:2]), (own[:2], other[:2])


def bits(es):
    return sum(1 << e for e in es)


def place(s, r):
    return s if s < r else s - 1


def place1(pos):
    return [p for group in EXPECTED for p in group].index(pos)


def share(es, calls, pos):
    call = [c for c in calls if pos in c][0]
    w, j = len(es) // len(call), call.index(pos)
    return es[w * j:w * j + w]


DC2 = (slice(0, 4), slice(4, 6), slice(6, 8))
DS2 = (slice(0, 2), slice(2, 4), slice(4, 8))


def landed(layer, s, r, T, topo):
    relayed, direct, help1, _ = plan(s, T, topo)
    if layer == 1:
        if r in relayed:
            return sum(len(topo.engines(h[relayed.index(r)], T.cores[r])) for h in help1)
        es = topo.engines(T.cores[s], T.cores[r])
        return sum(len(share(es, calls, 4 + direct.index(r))) for calls in (CODE_CALLS, PLANE_CALLS))
    if r in relayed:
        return 8
    j = direct.index(r)
    return DC2[j].stop - DC2[j].start + DS2[j].stop - DS2[j].start


def b8(v):
    return v.bitcast(dt.uint8)


def runs(order):
    out = []
    for p, r in enumerate(order):
        if out and out[-1][1] + out[-1][2] == r:
            out[-1][2] += 1
        else:
            out.append([p, r, 1])
    return out


def rank_program(g, core, T, topo):
    rank = T.rank_of(core)
    S = T.sem
    if rank is None:
        for c in topo.cores_of(core):
            s = T.rank_of(c)
            if s is not None:
                helper(g, core, s, T, topo)
        return
    relayed, direct, help1, help2 = plan(rank, T, topo)
    order = relayed + direct
    V, P, A, Y = g.vector, g.tensor, g.scalar, g.sync
    mult, add, mx = AluOpType.mult, AluOpType.add, AluOpType.max
    COPY, RELU = ActivationFunctionType.Copy, ActivationFunctionType.Relu
    seen = {}

    def need(eng, name, sem, n):
        if seen.get((name, sem), 0) < n:
            eng.wait_ge(S[sem], n)
            seen[(name, sem)] = n

    def gather(eng, out, win, sem):
        if eng is V:
            V.tensor_copy(out, win).then_inc(S[sem], 1)
        else:
            A.activation(out, win, COPY).then_inc(S[sem], 1)

    for q, e in enumerate((A, Y, A, Y)):
        e.dma_start(T.ls1[16 * q:16 * q + 16, :], T.snd1[:, :]).then_inc(S.ds1, 16)
    Y.dma_start(T.xt[:, PAD:], T.x[:]).then_inc(S.dx, 16)
    Y.dma_start(T.w1t[:], T.w1[:]).then_inc(S.dw1, 16)
    Y.dma_start(T.lmix[0:16, 0:64], T.src1[:, :]).then_inc(S.dl, 16)
    n = 1
    for u in range(4):
        Y.dma_start(T.lsrc[4 * u:4 * u + 4, 4 - u:260 - u], T.src1[:, :]).then_inc(S.dl, 16)
        Y.dma_start(T.lsrc[4 * u:4 * u + 4, 260 - u:388 - u], T.src2[:, :]).then_inc(S.dl, 16)
        n += 2
    for p, r, w in runs(order):
        Y.dma_start(T.lmix[0:16, 64 + 2 * p:64 + 2 * (p + w)], T.snd2[:, 2 * r:2 * (r + w)]).then_inc(S.dl, 16)
        n += 1
    nlists = 16 * n
    Y.dma_start(T.w2t[:], T.w2[:]).then_inc(S.dw2, 16)
    Y.wait_ge(S.lo, 3)
    for q in range(1, 8):
        Y.dma_start(T.ol[16 * q:16 * q + 16, 0:OEND], T.ol[0:16, 0:OEND]).then_inc(S.dr, 16)

    V.memset(T.xt[:, 0:PAD], 0.0).then_inc(S.mp, 1)
    V.memset(T.m1[:], 1.0).then_inc(S.mk, 1)
    A.wait_ge(S.ml, 1)
    for t in range(4):
        a = t * WP + NT + rank * C1
        A.activation(T.wz[:, a:a + C1], T.m1[:, 0:C1], COPY).then_inc(S.mz, 1)
    V.memset(T.uz[:, NT + rank * C2:NT + rank * C2 + C2], 0.0).then_inc(S.mz, 1)
    V.memset(T.hg[:, 4 * 7 * C2:1024], 0.0).then_inc(S.mz, 1)
    V.wait_ge(S.mk, 1)
    V.memset(T.m1[:, 0:2 * NT:4], 0.0).then_inc(S.ml, 1)

    V.wait_ge(S.ds1, 64)
    V.tensor_copy(T.ls1[64:128, :], T.ls1[0:64, :]).then_inc(S.lq, 1)
    V.wait_ge(S.lq, 1)
    for t in range(4):
        V.tensor_scalar(T["of%d" % t][:], T.ls1[:], 4, PAD + t, mult, add).then_inc(S["of%d" % t], 1)

    for e in (A, V):
        e.wait_ge(S.mp, 1)
        e.wait_ge(S.dx, 16)
    for turn, pos in enumerate(SEQUENCE):
        r = order[pos]
        for t in range(4):
            eng, name = (A, "A") if t < 4 - VECTOR_GATHERS[turn] else (V, "V")
            need(eng, name, "of%d" % t, 1)
            gather(eng, T.xg[:, 4 * C1 * pos + t:4 * C1 * (pos + 1):4],
                   T.xt[:, :].indirect(T["of%d" % t][:, 10 * r:10 * r + 10]), "xg%d" % pos)
        call = [c for c in CODE_CALLS if pos in c][0]
        if turn == 3:
            V.wait_ge(S.dl, nlists)
            V.tensor_copy(T.ol[0:16, O1E:O1N], T.lsrc[0:16, 4:388:4]).then_inc(S.lo, 1)
            V.tensor_copy(T.ol[0:16, O1N:OS4], T.lmix[0:16, 0:78]).then_inc(S.lo, 1)
            V.tensor_scalar(T.ol[0:16, OS4:OEND], T.lmix[0:16, 64:78], 0, 4, mx, mult).then_inc(S.lo, 1)
        if turn == 4:
            V.wait_ge(S.dw1, 16)
            V.quantize_mx(T.w1q[:, 0:256], T.w1s[:, 0:256], T.w1t[:, 0:1024]).then_inc(S.w1a, 1)
        if turn == 5:
            V.quantize_mx(T.xq[:], T.xs[:], T.xt[:, PAD:]).then_inc(S.xo, 1)
        if pos == call[-1]:
            for p in call:
                V.wait_ge(S["xg%d" % p], 4)
            a, b = C1 * call[0], C1 * (pos + 1)
            V.quantize_mx(T.xgq[:, a:b], T.xgs[:, a:b], T.xg[:, 4 * a:4 * b]).then_inc(S["xq%d" % pos], 1)

    V.quantize_mx(T.w1q[:, 256:512], T.w1s[:, 256:512], T.w1t[:, 1024:2048]).then_inc(S.w1b, 1)

    def sender(pos):
        for s in range(N):
            if s != rank:
                rl, di, _, _ = plan(s, T, topo)
                if (rl + di)[pos] == rank:
                    return s

    freed = [0, 0]
    for k in range(1 + len(EXPECTED)):
        if k == 0:
            P.wait_ge(S.xo, 1)
            n, parts, mq, ms = NT, [(0, NT)], T.xq[:], T.xs[:]
            planes, scalar = (0, 1, 2, 3), (0, 1, 2)
        else:
            group = EXPECTED[k - 1]
            for pos in group:
                P.wait_ge(S["arr1_%d" % sender(pos)], landed(1, sender(pos), rank, T, topo))
            a, n = C1 * place1(group[0]), C1 * len(group)
            parts, mq, ms = [(NT + C1 * sender(pos), C1) for pos in group], T.aq1[:, a:a + n], T.as1[:, a:a + n]
            planes, scalar = ((0, 2, 1, 3), (0, 1)) if k < len(EXPECTED) else ((0, 1, 2, 3), (0,))
        for i in planes:
            need(P, "P", "w1a" if i < 2 else "w1b", 1)
            bank = 512 * (4 * (k % 2) + i)
            done, free = "mm%d_%d" % (i, k % 2), "fr%d_%d" % (i, k % 2)
            if k >= 2:
                P.wait_ge(S[free], freed[k % 2])
            P.matmul_mx(T.ps[:, bank:bank + n], T.w1q[:, 128 * i:128 * i + 128], T.w1s[:, 128 * i:128 * i + 128],
                        mq, ms, True, True).then_inc(S[done], 1)
            (A if i in scalar else V).wait_ge(S[done], k // 2 + 1)
            for j, (base, w) in enumerate(parts):
                out, res = T.wz[:, WP * i + base:WP * i + base + w], T.ps[:, bank + w * j:bank + w * j + w]
                if i in scalar:
                    A.activation(out, res, RELU, scale=0.05).then_inc(S[free], 1)
                else:
                    V.tensor_scalar(out, res, 0.05, 0.0, mult, mx).then_inc(S[free], 1)
        freed[k % 2] += len(parts)

    for e in (V, A):
        e.wait_ge(S.mz, 6)
        e.wait_ge(S.dr, 112)
        e.wait_ge(S.lo, 3)
    V.wait_ge(S.ml, 1)

    def plane(eng, name, t):
        for b in range(2):
            need(eng, name, "fr%d_%d" % (t, b), freed[b])
        return T.wz[:, WP * t:WP * (t + 1)]

    def step(t, e):
        if t > 1:
            return T.sc[:, SP * (t - 2) + PAD:SP * (t - 2) + PAD + 4 * NT:4]
        return T.mx[:, NT * (4 * t + e):NT * (4 * t + e + 1)]

    def first(t):
        gather(A, step(t, 0), plane(A, "A", t).indirect(T.ol[:, O1E:O1E + 16]), "f%d_0" % t)

    def more(t, e):
        win = plane(V, "V", t).indirect(T.ol[:, O1E + 16 * e:O1E + 16 * e + 16])
        V.wait_ge(S["f%d_%d" % (t, e - 1)], 1)
        V.tensor_tensor(step(t, e), win, step(t, e - 1), mx).then_inc(S["f%d_%d" % (t, e)], 1)

    def four(t, a, b, sem):
        o = 4 * NT * (t - 2)
        gather(A, T.gt[:, o + a:o + b], plane(A, "A", t).indirect(T.ol[:, O1N + a // 16:O1N + b // 16]), sem)

    def scan(t, a, b, sem):
        o, p = 4 * NT * (t - 2), SP * (t - 2) + PAD - 3
        need(V, "V", sem, 1)
        V.tensor_tensor_scan(T.sc[:, p + a:p + b], T.m1[:], T.gt[:, o + a:o + b], 0.0, mult,
                             mx).then_inc(S["f%d_3" % t], 1)

    def chosen(eng, name, t, a, b, sem):
        need(eng, name, "f%d_3" % t, 2 if t > 1 else 1)
        o = SP * (t - 2) + PAD
        win, of = (step(t, 3), OS2) if t < 2 else (T.sc[:, o:o + 4 * NT - 3], OS4)
        gather(eng, T.hg[:, 4 * a + t:4 * b:4], win.indirect(T.ol[:, of + a // 16:of + b // 16]), sem)

    first(0)
    first(1)
    four(2, 0, 1024, "g2")
    four(3, 0, 512, "g3a")
    four(3, 512, 1024, "g3b")
    for t in (0, 1):
        chosen(A, "A", t, 0, 7 * C2, "cf")
    chosen(A, "A", 3, 128, 7 * C2, "cd")

    for e in (1, 2, 3):
        more(0, e)
        more(1, e)
    scan(2, 0, 512, "g2")
    scan(2, 512, 1024, "g2")
    scan(3, 0, 512, "g3a")
    chosen(V, "V", 2, 0, 7 * C2, "cf")
    scan(3, 512, 1024, "g3b")
    chosen(V, "V", 3, 0, 128, "cf")
    V.wait_ge(S.cf, 4)
    V.quantize_mx(T.hgq[:, 0:128], T.hgs[:, 0:128], T.hg[:, 0:512]).then_inc(S.hqr, 1)
    V.wait_ge(S.cd, 1)
    V.quantize_mx(T.hgq[:, 128:256], T.hgs[:, 128:256], T.hg[:, 512:1024]).then_inc(S.hqd, 1)

    A.activation(T.ht[:, 0:4 * NT:4], step(0, 3), COPY).then_inc(S.hc, 1)
    for t in (1, 2, 3):
        need(V, "V", "f%d_3" % t, 2 if t > 1 else 1)
        V.tensor_copy(T.ht[:, t:4 * NT:4], step(t, 3)).then_inc(S.hc, 1)
    V.wait_ge(S.dw2, 16)
    V.quantize_mx(T.w2q[:], T.w2s[:], T.w2t[:]).then_inc(S.w2r, 1)
    V.wait_ge(S.hc, 4)
    V.quantize_mx(T.htq[:], T.hts[:], T.ht[:]).then_inc(S.hor, 1)

    for i in range(4):
        for b in range(2):
            P.wait_ge(S["fr%d_%d" % (i, b)], freed[b])
    P.wait_ge(S.w2r, 1)
    P.wait_ge(S.hor, 1)
    P.matmul_mx(T.ps[:, 0:NT], T.w2q[:], T.w2s[:], T.htq[:], T.hts[:], True, True).then_inc(S.m2o, 1)
    V.wait_ge(S.m2o, 1)
    V.tensor_copy(T.uz[:, 0:NT], T.ps[:, 0:NT]).then_inc(S.ud, 1)
    for s in range(N):
        if s != rank:
            P.wait_ge(S["arr2_%d" % s], landed(2, s, rank, T, topo))
    P.matmul_mx(T.ps[:, 2048:2176], T.w2q[:], T.w2s[:], T.aq2[:, 0:128], T.as2[:, 0:128], True, True).then_inc(S.m2a, 1)
    P.matmul_mx(T.ps[:, 2560:2688], T.w2q[:], T.w2s[:], T.aq2[:, 96:224], T.as2[:, 96:224], True, True).then_inc(S.m2b, 1)
    A.wait_ge(S.m2a, 1)
    V.wait_ge(S.m2b, 1)
    done, hole = 1, C2 * rank
    for a, b, bank in ((0, 112, 2048), (112, 224, 2560 - 96)):
        for lo, hi in ((a, min(b, hole)), (max(a, hole), b)):
            if lo < hi:
                o = NT + lo + (C2 if lo >= hole else 0)
                out, res = T.uz[:, o:o + hi - lo], T.ps[:, bank + lo:bank + hi]
                if a == 0:
                    A.activation(out, res, COPY).then_inc(S.ud, 1)
                else:
                    V.tensor_copy(out, res).then_inc(S.ud, 1)
                done += 1

    V.wait_ge(S.ud, done)
    A.wait_ge(S.ud, done)

    def src(e):
        return T.uz[:, :].indirect(T.ol[:, O2E + 8 * e:O2E + 8 * e + 8])

    def part(e):
        return T.gu[:, TG * e:TG * e + TG]

    gather(A, part(0), src(0), "u0")
    gather(V, part(1), src(1), "u1")
    V.wait_ge(S.u0, 1)
    V.tensor_tensor(part(2), src(2), part(0), mx).then_inc(S.u2, 1)
    V.wait_ge(S.u1, 1)
    V.tensor_tensor(part(3), src(3), part(1), mx).then_inc(S.u3, 1)
    V.wait_ge(S.u2, 1)
    V.wait_ge(S.u3, 1)
    V.tensor_tensor(T.yt[:], part(2), part(3), mx).then_inc(S.yc, 1)
    Y.wait_ge(S.yc, 1)
    Y.dma_start(T.y[:], T.yt[:]).then_inc(S.ys, 16)
    Y.wait_ge(S.ys, 16)

    sent = [0]

    def fused(parts):
        ts = []
        for d, es, src, dst, sem in parts:
            rid, pid = topo.addr(d, core)
            ts.append(RemoteDMATransfer(dst_ids=[DstId(rid=rid, pnc=pid)], dma_engine_mask=bits(es), remote_sem=sem,
                                        src=src, dst=dst))
            sent[0] += len(es)
        g.remote_dma_fused(ts, local_sem=S.sent)

    def piece(pos, code):
        a, r = C1 * pos, order[pos]
        if pos < 4:
            d = help1[0 if code else 1][pos]
            j = help1[0 if code else 1][:pos].count(d)
            o, sem, dq, ds = C1 * j, S[("rc1" if code else "rs1") + "ab"[j]], T.hq1, T.hs1
        else:
            d = T.cores[r]
            o, sem, dq, ds = C1 * place1(pos), S["arr1_%d" % rank], T.aq1, T.as1
        es = share(topo.engines(core, d), CODE_CALLS if code else PLANE_CALLS, pos)
        if code:
            return d, es, b8(T.xgq[:, a:a + C1]), b8(dq[:, o:o + C1]), sem
        return d, es, T.xgs[:, a:a + C1], ds[:, o:o + C1], sem

    for last in [p for p in SEQUENCE if p in [c[-1] for c in CODE_CALLS]]:
        g.wait_ge(S["xq%d" % last], 1)
        for code, calls in ((True, CODE_CALLS), (False, PLANE_CALLS)):
            for call in calls:
                if call[-1] == last:
                    fused([piece(pos, code) for pos in call])

    g.wait_ge(S.hqr, 1)
    for code in (True, False):
        parts = []
        for j, d in enumerate(help2[0 if code else 1]):
            es = topo.engines(core, d)
            es = es[len(es) // 2 * j:len(es) // 2 * (j + 1)]
            a = 2 * C2 * j
            if code:
                parts.append((d, es, b8(T.hgq[:, a:a + 2 * C2]), b8(T.hq2[:, :]), S.r2))
            else:
                parts.append((d, es, T.hgs[:, a:a + 2 * C2], T.hs2[:, :], S.r2s))
        fused(parts)
    g.wait_ge(S.hqd, 1)
    codes, planes = [], []
    for j, r in enumerate(direct):
        d = T.cores[r]
        es = topo.engines(core, d)
        a, o = C2 * (4 + j), C2 * place(rank, r)
        sem = S["arr2_%d" % rank]
        codes.append((d, es[DC2[j]], b8(T.hgq[:, a:a + C2]), b8(T.aq2[:, o:o + C2]), sem))
        planes.append((d, es[DS2[j]], T.hgs[:, a:a + C2], T.as2[:, o:o + C2], sem))
    fused(codes)
    fused(planes)
    g.wait_ge(S.sent, sent[0])


def helper(g, core, s, T, topo):
    relayed, _, help1, help2 = plan(s, T, topo)
    S = T.sem
    me = T.cores[s]
    mine = topo.engines(me, core)
    sent = 0
    for pos in range(4):
        for code in (True, False):
            by = help1[0 if code else 1]
            if by[pos] != core:
                continue
            j = by[:pos].count(core)
            d = T.cores[relayed[pos]]
            o, a = C1 * place1(pos), C1 * j
            rid, pid = topo.addr(d, core)
            if code:
                sem, calls, out, src = "rc1", CODE_CALLS, b8(T.aq1[:, o:o + C1]), b8(T.hq1[:, a:a + C1])
            else:
                sem, calls, out, src = "rs1", PLANE_CALLS, T.as1[:, o:o + C1], T.hs1[:, a:a + C1]
            g.wait_ge(S[sem + "ab"[j]], len(share(mine, calls, pos)))
            g.remote_dma(out, src, S["arr1_%d" % s], S.sent, pid, rid, topo.mask(core, d))
            sent += len(topo.engines(core, d))
    for code in (True, False):
        if core not in help2[0 if code else 1]:
            continue
        j = help2[0 if code else 1].index(core)
        g.wait_ge(S.r2 if code else S.r2s, len(mine) // 2)
        ts = []
        for i, r in enumerate(relayed[2 * j:2 * j + 2]):
            d = T.cores[r]
            es = topo.engines(core, d)[4 * i:4 * i + 4]
            o, a = C2 * place(s, r), C2 * i
            src = b8(T.hq2[:, a:a + C2]) if code else T.hs2[:, a:a + C2]
            dst = b8(T.aq2[:, o:o + C2]) if code else T.as2[:, o:o + C2]
            rid, pid = topo.addr(d, core)
            ts.append(RemoteDMATransfer(dst_ids=[DstId(rid=rid, pnc=pid)], dma_engine_mask=bits(es),
                                        remote_sem=S["arr2_%d" % s], src=src, dst=dst))
            sent += len(es)
        g.remote_dma_fused(ts, local_sem=S.sent)
    if sent:
        g.wait_ge(S.sent, sent)
